import numpy as np, ml_dtypes
CORES = [3,11,19,27,35,43,51,59]
N = 8
BF = ml_dtypes.bfloat16
W, P, RO, L = 2048, 2, 4, 256
Q = 0.673
def parts(rng):
    share = rng.choice(np.array([0.015, 0.025, 0.04]), (N, 8, 1, 1)) * Q
    r = np.where(rng.random((N, 8, 16, W)) < share, rng.integers(5, 16, (N, 8, 16, W)), rng.integers(0, 5, (N, 8, 16, W)))
    hot = (rng.random((N, 8, 1, W)) < 0.004 * Q) & (rng.random((N, 8, 16, W)) < 0.7)
    r = np.where(hot, 15, r)
    return r, rng.integers(0, 256, (N, 8, 16, W)), rng.integers(0, W, (N, 8, 16, W)), rng.integers(0, W, (N, 8, 16, L))
def pack(r, x, k, s):
    return {"rec": np.ascontiguousarray(r.reshape(N, 128, W)).astype(np.float32).astype(BF), "wealth": np.ascontiguousarray(x.reshape(N, 128, W)).astype(np.float32).astype(BF),
            "kin": np.ascontiguousarray(k.reshape(N, 128, W)).astype(np.int32), "slips": np.ascontiguousarray(s.reshape(N, 128, L)).astype(np.int32)}
def setup_inputs(rng):
    r, x, k, s = parts(rng)
    return pack(r, x, k, s)
def setup_inputs_spread(rng):
    e = np.exp2(4.3 + 3.9 * rng.random((N, 8, 16, 1))) / Q
    r = np.minimum((16 * rng.random((N, 8, 16, W)) ** e).astype(np.int64), 15)
    x = np.minimum((np.exp2(8 * rng.random((N, 8, 1, W))) * rng.random((N, 8, 16, W))).astype(np.int64), 255)
    k = np.minimum((W * rng.random((N, 8, 16, W)) ** 2).astype(np.int64), W - 1)
    s = np.minimum((W * rng.random((N, 8, 16, L)) ** (1 + rng.random((N, 8, 1, L)))).astype(np.int64), W - 1)
    return pack(r, x, k, s)
def setup_inputs_ends(rng):
    r = 15 * (rng.random((N, 8, 16, W)) < 0.02 * Q)
    r = np.where(rng.random((N, 8, 1, W)) < 0.004 * Q, 15, r)
    w = rng.random((N, 8, 1, W)); x = 255 * np.where(w < 0.4, 0, np.where(w < 0.7, 1, rng.integers(0, 2, (N, 8, 16, W))))
    u = rng.random((N, 8, 16, W))
    k = np.where(u < 0.36, 0, np.where(u < 0.72, W - 1, np.where(u < 0.78, W - 2, rng.integers(0, W, (N, 8, 16, W)))))
    for first, places in ((1, ((2, W - 2), (15, W - 1))), (3, ((4, W - 1), (9, 5), (12, 5))), (6, ((4, 5), (9, W - 1)))):
        c = np.zeros((16, 1), np.int64)
        for m, v in places: c[m, 0] = v
        k[:, :, :, first::8] = c; x[:, :, :, first::8] = 0
    m = (np.arange(W) & 4) == 4
    k[:, 7] = np.where(m & (k[:, 7] == W - 1), 0, k[:, 7])
    a, b = W - 600, W - 344
    k[:, :, :, a:b] = 0; r[:, :, :, a:b] = 0; x[:, :, :, a:b] = 0
    k[:, :, :, W - 40:W - 24] = 0; r[:, :, :, W - 40:W - 24] = 0; x[:, :, :, W - 40:W - 24] = 0; k[:, :, 15, W - 32:W - 24] = W - 1
    r[:, :, :, 0] = 0; r[:, :, :, W - 1] = 15 * (rng.random((N, 8, 16)) < rng.choice(np.array([0.05, 0.15, 0.3]), (N, 8, 1))); r[:, 7, :, W - 1] = 15
    r[:, :, :, W - 2] = 0; r[:, :, :, 5] = 0
    x[:, :, :, 0] = 0; x[:, :, :, W - 1] = 255; x[:, :, :, 5] = 255; x[:, :, :, W - 2] = 255; x[:, :, 15, W - 2] = 254
    u = rng.random((N, 8, 16, L)); s = np.where(u < 0.35, 0, np.where(u < 0.7, W - 1, rng.integers(1, W - 600, (N, 8, 16, L))))
    s[:, :, :, 112:128] = W - 1
    for q in range(2):
        for g in range(8): s[q, g, :, 240:] = a + rng.permutation(256).reshape(16, 16)
    p = np.arange(16); s[N - 1, 7, :, 255] = np.where((p & 1) == 0, W - 40 + (p >> 1), W - 32 + (p >> 1))
    return pack(r, x, k, s)
def setup_inputs_corners(rng):
    r, x, k, s = parts(rng); own = np.arange(W); lane = np.arange(L)
    k[:, :4] = own
    n = rng.choice(np.array([0, 1, 3, 7, 8, 9, 11, 12, 13, 16]), (1, 4, 1, W)); order = np.argsort(rng.random((1, 4, 16, W)), axis=2)
    high = np.where(rng.random((N, 4, 16, W)) < 0.7, 15, rng.integers(6, 16, (N, 4, 16, W)))
    low = np.where(rng.random((N, 4, 16, W)) < 0.15, 5, rng.integers(0, 5, (N, 4, 16, W)))
    high[:, 1] = 6; low[:, 1] = 5; high[:, 2] = 6 + (own & 7); low[:, 2] = 5 + (own & 7)
    r[:, :4] = np.where(order < n, high, low)
    s[:, :2] = lane + 256 * rng.integers(0, W // 256, (N, 2, 16, L))
    s[:, 4] = np.repeat(rng.integers(0, W, (N, 1, 16)), 16, axis=2)
    for q in range(N):
        if (q & 1) == 0: s[q, 5] = rng.integers(0, W)
        else: s[q, 5] = lane + 256 * rng.integers(0, W // 256, (16, L))
    k[:, 6] = rng.choice(np.array([0, W - 1, W // 2]), (N, 1, W))
    z = rng.integers(0, 3, (N, 16, W)); k[:, 7] = np.where(z == 0, 0, np.where(z == 1, W - 1, own))
    r[:, 6:, :, [0, W - 1, W // 2]] = np.where(rng.random((N, 2, 16, 3)) < 0.2, 15, rng.integers(0, 5, (N, 2, 16, 3)))
    s[:, 7] = np.where(rng.random((N, 16, L)) < 0.1, rng.choice(np.array([0, W - 1]), (N, 16, L)), s[:, 7])
    x[:, 1] = 255; x[:, 2] = 255 * rng.integers(0, 2, (N, 1, W))
    return pack(r, x, k, s)
def setup_inputs_alike(rng):
    r, x, k, s = parts(rng)
    pool = np.repeat(rng.integers(0, W, (N, 8, 16, 6)), 16, axis=2)
    few = np.take_along_axis(pool, rng.integers(0, 6, (N, 8, L, 16)), 3).transpose(0, 1, 3, 2)
    s[:, ::2] = few[:, ::2]
    s[:, 1::4, :, 1::2] = np.roll(s[:, 1::4, :, 0::2], 5, axis=2)
    s[:, 3] = W - 1 - rng.integers(0, 40, (N, 16, L))
    k[:, 1::2, 8:] = k[:, 1::2, :8]
    x = np.take_along_axis(rng.choice(np.array([0, 128, 255]), (N, 8, 16, 5)), rng.integers(0, 5, (N, 8, 1, W)), 3)
    return pack(r, x, k, s)
def setup_inputs_full(rng):
    r, x, k, s = parts(rng); own = np.arange(W); lane = np.arange(L); bag = (own >> 4) & 15
    z = 2 * rng.integers(0, 8, N) + 1
    r[:, :3] = rng.integers(0, 5, (N, 3, 16, W))
    even = own[(own & 16) == 0]; r[:, 1, bag[even], even] = 15; k[:, 1] = k[:, 1] | 16
    hot = np.repeat((bag[None, :] == z[:, None])[:, None, :], 8, axis=1)
    hot[:, :2, :256] = False; hot[:, 2, :256:2] = False
    r = np.where(hot[:, :, None, :], 15, r)
    named = np.take_along_axis(hot, k.reshape(N, 8, 16 * W), 2).reshape(N, 8, 16, W); k = np.where(named, k ^ 32, k)
    s[:, :3] = lane + 256 * rng.integers(0, W // 256, (N, 3, 16, L))
    inbag = (lane >> 4)[None, :] == z[:, None]
    first = np.arange(16)[:, None] == ((5 * (lane & 15)) & 15)[None, :]
    s = np.where(inbag[:, None, None, :], lane + 256 * np.where(first, 0, rng.integers(1, W // 256, (N, 8, 16, L))), s)
    return pack(r, x, k, s)
def check_inputs(d):
    bad = []
    for k, lo, hi in (("rec", 0, 15), ("wealth", 0, 255), ("kin", 0, W - 1), ("slips", 0, W - 1)):
        v = np.asarray(d[k]).astype(np.float64)
        if not (np.min(v) >= lo and np.max(v) <= hi): bad.append("range of " + k)
        elif np.any(v != np.floor(v)): bad.append("whole numbers of " + k)
    return bad
def reference(rec, wealth, kin, slips):
    R = rec.astype(np.float32).astype(np.int64).reshape(N, 8, 16, W); X = wealth.astype(np.float32).astype(np.int64).reshape(N, 8, 16, W)
    K = kin.astype(np.int64).reshape(N, 8, 16, W); S = slips.astype(np.int64).reshape(N, 8, 16, L)
    lane = np.arange(L); b = lane >> 4; j = lane & 15; a = np.zeros((N, 16), np.int64)
    lower = lane[None, :] < lane[:, None]
    def picks(tab, ks):
        return np.take_along_axis(tab, ks.reshape(8, 1, 16 * L), 2).reshape(8, 16, 16, L)
    for t in range(RO):
        T = 8 + t; later = []
        for r in range(N):
            o = (a[r][b] + 5 * j + t) & 15
            c = S[r][:, o, lane]
            ci = c[:, None, :]
            counts = ~np.any((c[:, :, None] == c[:, None, :]) & lower[None], axis=2)
            kc = np.take_along_axis(K[r], ci, 2)
            M = np.maximum(np.take_along_axis(R[r], ci, 2), np.max(picks(R[r], kc), axis=2))
            for u in range(P):
                q = (r + 1 + (P * t + u) % (N - 1)) % N
                M = np.maximum(M, np.max(picks(R[q], np.take_along_axis(K[q], ci, 2)), axis=2))
            f = np.sum(M >= T - 2, axis=1)
            bar = (M[:, b, lane] >= T - 3) | (f >= 8)
            barred = counts & bar; inst = counts & ~bar
            torn = inst | (barred & (f >= 12))
            nxt = np.zeros((8, L), bool); nxt[:, :L - 16] = torn[:, 16:]
            moved = barred & (f < 12) & ((f & 1) == 1) & nxt
            sc = np.sum(np.maximum(picks(X[r], kc) - np.take_along_axis(X[r], ci, 2)[:, :, None, :], 0), axis=1)
            best = np.take_along_axis(kc, np.argmax(sc, axis=1)[:, None, :], 1)[:, 0]
            new = np.where(torn | moved, best, c)
            new[:, 16:] = np.where(moved[:, :L - 16], c[:, :L - 16], new[:, 16:])
            later.append((o, c, inst, new))
        for r in range(N):
            o, c, inst, new = later[r]
            S[r][:, o, lane] = new
            gi, li = np.nonzero(inst)
            R[r][gi, b[li], c[gi, li]] = T
            K[r][gi, t, c[gi, li]] = c[gi, li ^ 1]
            a[r] = np.sum(inst.reshape(8, 16, 16), axis=(0, 2))
    return {"yr": R.reshape(N, 128, W).astype(np.float32).astype(BF), "ys": S.reshape(N, 128, L).astype(np.float32)}

@@ -1,0 +1,521 @@
+import math
+from concourse.bass import DstId, RemoteDMATransfer
+from concourse.mybir import dt, AluOpType as Op, ActivationFunctionType as Fn
+
+NR, RO, W, L = 8, 4, 2048, 256
+WX = W + L
+NCH, CH = 4, 64
+V_ASK = (0, 1)
+OWN_LAST = (3,)
+
+SCRATCH = {}
+
+
+def _s(name, cols, dtype="float32", where="sbuf"):
+    SCRATCH[name] = (where, [128, cols], dtype)
+
+
+for _n in ("E", "R"):
+    _s(_n, WX, "bfloat16")
+_s("X", W, "bfloat16")
+_s("K", WX, "int32")
+_s("SN", L, "int32")
+_s("SF", L)
+_s("IDX", W)
+for _n in ("GO", "GA0", "GA1", "Y", "XR"):
+    _s(_n, 16 * L, "bfloat16")
+for _n in ("KL", "AK0", "AK1"):
+    _s(_n, L, "uint16")
+_s("EQ", 2176, "bfloat16")
+LOG = {}
+
+
+def _many(base, names, cols, dtype="float32"):
+    _s(base, cols * len(names), dtype)
+    for i, n in enumerate(names):
+        LOG[n] = (base, cols * i, cols)
+
+
+_TT = range(RO)
+_TK = [(t, k) for t in range(RO) for k in range(2)]
+_many("CLB", ["CL%d" % t for t in _TT], 16, "uint16")
+_many("RQB", ["RQ%d%d" % x for x in _TK], 16, "uint16")
+_many("RSB", ["RS%d%d" % x for x in _TK], L, "bfloat16")
+_many("ASB", ["AS%d%d" % x for x in _TK], L, "bfloat16")
+_many("BMB", ["BM%d" % t for t in _TT], L)
+_many("BTB", ["BT%d" % t for t in _TT], L, "bfloat16")
+_many("TBF", ["TB%d" % t for t in _TT], L, "bfloat16")
+_many("ISB", ["IST%d" % t for t in _TT], 1)
+_many("NOB2", ["NOT%d" % t for t in _TT], 1)
+_many("CSB", ["CST%d" % t for t in _TT], 2, "bfloat16")
+_many("PLB", ["PL%d" % t for t in _TT], 2)
+for _n in ("CREP", "KCF", "KVA", "CSW", "KV", "RM", "NI", "DK", "BK", "MS", "CS", "LH", "LH2", "XS", "RST", "JF", "BF", "DG", "NOB", "OB"):
+    _s(_n, L)
+for _n in ("RCE", "NVR", "MK0", "MK1", "NTH", "CK"):
+    _s(_n, L, "bfloat16")
+for _n in ("UT", "VT", "NT"):
+    _s(_n, L + 32, "bfloat16")
+_s("D", L, "int32")
+_s("D15", L, "int32")
+_s("CB", 128, "int32")
+for _n in ("IDF", "IDS", "SH", "SHW", "PSW"):
+    _s(_n, 128)
+for _n in ("IDB", "BD", "W1", "W2", "O128", "IOS"):
+    _s(_n, 128, "bfloat16")
+_s("GF", 8)
+_s("G8", 8, "int32")
+for _n in ("GB", "GB4", "GB16", "GB32"):
+    _s(_n, 8, "bfloat16")
+_s("PC", 2, "int32")
+_s("PM", 2, "int32")
+_s("SMI", 8, "int32")
+_s("PMF", 2)
+_s("PGF", 1)
+_s("SG", 1)
+_s("P15", 1, "bfloat16")
+_s("EXI", 16, "int32")
+_s("EXP", 16, "uint16")
+_s("SW", 16, "uint16")
+_s("SL", 16, "uint16")
+for _n in ("LIX", "LWB", "LW", "CWF", "CC", "DD", "SLM", "BKF", "DL", "DL1", "P2", "ED"):
+    _s(_n, 16)
+_s("D12", 32)
+_s("RMV", 32)
+_s("P1", 32)
+_s("RR", 2)
+_s("EQP", 2)
+_s("C48", 48, "bfloat16")
+_s("I48", 48, "bfloat16")
+for _n in ("FI", "Q1", "Q2"):
+    _s(_n, 48, "int32")
+for _n in ("TBB", "TORN", "OBB", "BO"):
+    _s(_n, 48)
+for _n in ("pZ", "pA0", "pA1", "pK", "pS", "pD", "pF", "pM"):
+    _s(_n, 512, "float32", "psum")
+
+SEMAPHORES = ["sv", "sa", "sp", "sq", "loc", "ldS", "ldK", "ldR", "ldX", "stR", "stS"]
+SEMAPHORES += ["rq%d%d" % (t, k) for t in range(RO) for k in range(2)] + ["rs%d%d" % (t, k) for t in range(RO) for k in range(2)]
+
+
+def rank_program(g, core, T, topo):
+    rank = T.rank_of(core)
+    if rank is None:
+        return
+    V, A, PE = g.vector, g.scalar, g.tensor
+    eng = {"v": V, "a": A, "p": PE, "q": g, "s": g.sync}
+    own = {"v": "sv", "a": "sa", "p": "sp", "q": "sq"}
+    cnt = {"v": 0, "a": 0, "p": 0, "q": 0}
+    known = {q: {} for q in eng}
+    snap = {}
+    res = {}
+
+    def need(q, tok):
+        s, n = tok
+        if known[q].get(s, 0) >= n:
+            return
+        eng[q].wait_ge(T.sem[s], n)
+        known[q][s] = n
+        for s2, n2 in snap.get(tok, {}).items():
+            if known[q].get(s2, 0) < n2:
+                known[q][s2] = n2
+
+    def entry(k):
+        if k not in res:
+            res[k] = {"w": None, "r": {}, "lw": {}}
+        return res[k]
+
+    def deps(q, reads, writes):
+        d = []
+        for k in reads:
+            e = entry(k)
+            if k[0] == "p":
+                for q2, tok in e["lw"].items():
+                    if not (q2 == q == "p"):
+                        d.append(tok)
+                d += [tok for q2, tok in e["r"].items() if q2 != q]
+            elif e["w"]:
+                d.append(e["w"])
+        for k in writes:
+            e = entry(k)
+            if k[0] == "p":
+                for m in ("lw", "r"):
+                    d += [tok for q2, tok in e[m].items() if not (q2 == q == "p")]
+            else:
+                if e["w"]:
+                    d.append(e["w"])
+                d += list(e["r"].values())
+        best = {}
+        for s, n in d:
+            best[s] = max(best.get(s, 0), n)
+        for s in best:
+            need(q, (s, best[s]))
+
+    def mark(q, tok, reads, writes):
+        for k in reads:
+            entry(k)["r"][q] = tok
+        for k in writes:
+            e = entry(k)
+            if k[0] == "p":
+                e["lw"][q] = tok
+            else:
+                e["w"] = tok
+                e["r"] = {}
+
+    def op(q, reads, writes, fn):
+        deps(q, reads, writes)
+        ins = fn()
+        cnt[q] += 1
+        tok = (own[q], cnt[q])
+        ins.then_inc(T.sem[own[q]], 1)
+        snap[tok] = dict(known[q])
+        mark(q, tok, reads, writes)
+        return tok
+
+    def landed(k, sem, n):
+        entry(k)["w"] = (sem, n)
+
+    def ts(o, i, s1, s2, op0, op1=None, rd=(), wr=None, q="v"):
+        (on, oa), (inn, ia) = o, i
+        if op1 is None:
+            f = lambda: V.tensor_scalar(oa, ia, s1, None, op0)
+        else:
+            f = lambda: V.tensor_scalar(oa, ia, s1, s2, op0, op1)
+        return op("v", [inn] + list(rd), [on], f)
+
+    def tt(o, i0, i1, o0, rd=()):
+        return op("v", [i0[0], i1[0]] + list(rd), [o[0]], lambda: V.tensor_tensor(o[1], i0[1], i1[1], o0))
+
+    def cp(o, i, rd=()):
+        return op("v", [i[0]] + list(rd), [o[0]], lambda: V.tensor_copy(o[1], i[1]))
+
+    def act(o, i, fn=Fn.Copy, rd=(), **kw):
+        return op("a", [i[0]] + list(rd), [o[0]], lambda: A.activation(o[1], i[1], fn, **kw))
+
+    def mms(bank, parts, rd):
+        def f():
+            last = None
+            for (oa, l, r, st, sp) in parts:
+                last = PE.matmul(oa, l, r, st, sp)
+            return last
+        return op("p", rd, [bank], f)
+
+    def ap(name, lo=0, hi=None):
+        base, o, n = LOG.get(name, (name, 0, SCRATCH[name][1][1] if name in SCRATCH else 0))
+        return T[base][:, o + lo:o + (n if hi is None else hi)]
+
+    def b(name, lo=0, hi=None):
+        return (name, ap(name, lo, hi))
+
+    def iota(name, pattern, base, cm, imp=False):
+        kw = {"allow_small_or_imprecise_dtypes": True} if imp else {}
+        return op("q", [], [name], lambda: g.iota(T[name][:], pattern, base, cm, **kw))
+
+    def fill(name, val):
+        return op("v", [], [name], lambda: V.memset(ap(name), val))
+
+    g.sync.dma_start(T.SN[:], T.slips[:]).then_inc(T.sem.ldS, 16)
+    A.dma_start(T.R[:, 0:W], T.rec[:]).then_inc(T.sem.ldR, 16)
+    g.sync.dma_start(T.K[:, 0:W], T.kin[:]).then_inc(T.sem.ldK, 16)
+    A.dma_start(T.X[:], T.wealth[:]).then_inc(T.sem.ldX, 16)
+    landed("SN", "ldS", 16)
+    landed("R", "ldR", 16)
+    landed("K", "ldK", 16)
+    landed("X", "ldX", 16)
+
+    iota("PC", [[0, 2]], 0, 1)
+    iota("D", [[1, L]], 0, -1)
+    iota("JF", [[0, 16], [1, 16]], 0, 0, True)
+    iota("EXI", [[1, 16]], 0, 0)
+    iota("G8", [[1, 8]], 0, 0)
+    ts(b("PM"), b("PC"), 15, None, Op.bitwise_and)
+    cp(b("PMF"), b("PM"))
+    ts(b("SMI", 0, 1), b("PC", 0, 1), 4, None, Op.arith_shift_right)
+    cp(b("PGF"), b("SMI", 0, 1))
+    ts(b("IDF"), b("D", 0, 128), 0.0, None, Op.is_equal)
+    ts(b("IDB"), b("D", 0, 128), 0.0, None, Op.is_equal)
+    for t in range(RO):
+        ts(b("CST%d" % t), b("PMF"), 5.0, t - 7.5, Op.mult, Op.add)
+    ts(b("IOS"), b("JF", 0, 128), -7.5, None, Op.add)
+    cp(b("EXP"), b("EXI"))
+    ts(b("D15"), b("D"), 15, None, Op.bitwise_and)
+    ts(b("DG"), b("D15"), 0.0, None, Op.is_equal)
+    ts(b("RST"), b("JF"), 1.0, None, Op.min)
+    ts(b("GF"), b("G8"), T.PGF[:, 0:1], None, Op.is_equal, rd=["PGF"])
+    cp(b("SF"), b("SN"))
+    S = ("pS", T.pS[:, 256:512])
+    mms("pS", [(T.pS[:, 256 + 128 * h:384 + 128 * h], T.SF[:, 128 * h:128 * h + 128], T.IDF[:], True, True) for h in range(2)], ["SF", "IDF"])
+
+    MAG = 1.5 * 2.0 ** 27
+    SWZ = {}
+
+    def place(t):
+        mk = "MK%d" % (t % 2)
+        ts(b("RR"), ("pF", T.pF[:, 64:66]), MAG, -MAG, Op.add, Op.add)
+        for h in range(2):
+            ts((mk, T[mk][:, 128 * h:128 * h + 128]), b("IOS"), T.RR[:, h:h + 1], T.pF[:, 64 + h:65 + h], Op.add, Op.is_equal, rd=["RR", "pF"])
+
+    def sel1(t):
+        mk = "MK%d" % (t % 2)
+        tt(b("MS"), S, b(mk), Op.mult)
+
+    def sel2(t):
+        op("v", ["RST", "MS"], ["CS"], lambda: V.tensor_tensor_scan(T.CS[:], T.RST[:], T.MS[:], 0.0, Op.mult, Op.add))
+        tt(b("PL%d" % t), ("pF", T.pF[:, 64:66]), b("RR"), Op.subtract)
+
+    def expand(out, src):
+        op("v", [src, "EXP", "DG"], [out], lambda: V.tensor_tensor(T[out][:], T[src][:].indirect(T.EXP[:]), T.DG[:], Op.mult))
+
+    def wrap(t):
+        mms("pM", [(T.pM[:, 16 + 8 * h:24 + 8 * h], T.LH[:, 128 * h:128 * h + 128], T.GF[:], True, True) for h in range(2)], ["LH", "GF"])
+
+    def send_list(t):
+        trs = []
+        n = 0
+        for k in range(2):
+            q = (rank + 1 + ((2 * t + k) % 7)) % NR
+            dst = T.cores[q]
+            es = topo.engines(core, dst)
+            half = len(es) // 2
+            m = 0
+            for e in es[k * half:(k + 1) * half]:
+                m |= 1 << e
+            rid, pid, _x = topo.addr(dst)
+            trs.append(RemoteDMATransfer(dst_ids=[DstId(rid=rid, pnc=pid)], dma_engine_mask=m, remote_sem=T.sem["rq%d%d" % (t, k)],
+                                         src=ap("CL%d" % t), dst=ap("RQ%d%d" % (t, k))))
+            a = T.cores[(rank - 1 - ((2 * t + k) % 7)) % NR]
+            landed("RQ%d%d" % (t, k), "rq%d%d" % (t, k), len(topo.engines(a, core)) // 2)
+            n += half
+        deps("q", ["CL%d" % t], [])
+        g.remote_dma_fused(trs, local_sem=T.sem.loc)
+        SWZ["loc"] = SWZ.get("loc", 0) + n
+
+    def send_sums(t, k):
+        asker = T.cores[(rank - 1 - ((2 * t + k) % 7)) % NR]
+        rid, pid, _x = topo.addr(asker)
+        deps("q", ["AS%d%d" % (t, k)], [])
+        g.remote_dma(ap("RS%d%d" % (t, k)), ap("AS%d%d" % (t, k)), T.sem["rs%d%d" % (t, k)], T.sem.loc, pid, rid, topo.mask(core, asker))
+        SWZ["loc"] += len(topo.engines(core, asker))
+        q = T.cores[(rank + 1 + ((2 * t + k) % 7)) % NR]
+        landed("RS%d%d" % (t, k), "rs%d%d" % (t, k), len(topo.engines(q, core)))
+
+    mms("pF", [(T.pF[:, 64:66], T.IDB[:], ap("CST0"), True, True)], ["IDB", "CST0"])
+    place(0)
+    sel1(0)
+    sel2(0)
+    cp(b("CC"), ("CS", T.CS[:, 15::16]))
+    expand("LH", "CC")
+    wrap(0)
+    cp(b("CL0"), ("pM", T.pM[:, 16:32]))
+    send_list(0)
+
+    iota("CB", [[1, 8], [0, 16]], 0, 0)
+    iota("BF", [[1, 16], [0, 16]], 0, 0, True)
+    iota("LIX", [[128, 2], [0, 8]], W, 1, True)
+    iota("LWB", [[16, 16]], W, 0, True)
+    iota("IDX", [[1, W]], 0, 0, True)
+    ln2 = math.log(2.0)
+    act(b("P15"), b("PMF", 0, 1), Fn.Exp, scale=-ln2, bias=15.0 * ln2)
+    act(b("NTH"), b("JF"), Fn.Exp, scale=-ln2, bias=16.0 * ln2)
+    act(("E", T.E[:, 0:W]), ("R", T.R[:, 0:W]), Fn.Exp, scale=6.0 * ln2)
+    ts(b("NTH"), b("NTH"), -1.0, None, Op.mult)
+    ts(b("BD"), b("CB"), T.PGF[:, 0:1], None, Op.is_equal, rd=["PGF"])
+    ts(b("W2"), b("BD"), T.P15[:, 0:1], None, Op.mult, rd=["P15"])
+    ts(b("W1"), b("BD"), 65536.0, None, Op.mult)
+    for nm, f in (("GB", 1.0), ("GB4", 4.0), ("GB16", 16.0), ("GB32", 32.0)):
+        ts(b(nm), b("GF"), f, None, Op.mult)
+    ts(b("IDS"), b("IDF"), 1.0 / 4096.0, None, Op.mult)
+    ts(b("SH"), b("D", 0, 128), 16.0, None, Op.is_equal)
+    ts(b("SHW"), b("D", 0, 128), -112.0, None, Op.is_equal)
+    ts(b("SMI", 1, 2), b("PC", 0, 1), 1, None, Op.bitwise_and)
+    ts(b("SG"), b("SMI", 1, 2), -2.0, 1.0, Op.mult, Op.add)
+    ts(b("PSW"), b("D", 0, 128), T.SG[:, 0:1], None, Op.is_equal, rd=["SG"])
+    ts(b("CK"), b("JF"), -1.0, 15.0, Op.mult, Op.add)
+    fill("O128", 1.0 / 128.0)
+    fill("C48", 4.0)
+    for nm, x in (("UT", 0.0), ("VT", 0.0), ("NT", 1.0)):
+        fill(nm, x)
+    ts(b("LW"), b("LWB"), T.PMF[:, 0:1], None, Op.add, rd=["PMF"])
+    ts(b("NOB"), b("BF"), T.PMF[:, 0:1], None, Op.not_equal, rd=["PMF"])
+    ts(b("OB"), b("BF"), T.PMF[:, 0:1], None, Op.is_equal, rd=["PMF"])
+    for t in range(RO):
+        ts(b("BM%d" % t), b("NOB"), 1e29, 64.0 ** (5 + t), Op.mult, Op.add)
+        if t < RO - 1:
+            ts(b("BT%d" % t), b("OB"), 64.0 ** (8 + t), None, Op.mult)
+            ts(b("IST%d" % t), b("PMF", 0, 1), float(t), None, Op.is_equal)
+            ts(b("NOT%d" % t), b("PMF", 0, 1), float(t), None, Op.not_equal)
+        ts(b("TB%d" % t), b("OB"), float(8 + t), None, Op.mult)
+
+    def rec_piece(q, G, lst, c):
+        o, off = T[G][:, 1024 * c:1024 * c + 1024], T[lst][:, CH * c:CH * c + CH]
+        key = "%s.%d" % (G, c)
+        if q == "a":
+            op("a", ["E", lst], [key], lambda: A.activation(o, T.E[:, 0:W].indirect(off), Fn.Copy))
+        else:
+            op("v", ["E", lst], [key], lambda: V.tensor_copy(o, T.E[:, 0:W].indirect(off)))
+
+    def rec_sum(bank, G, c, whole):
+        parts = []
+        for m in range(16):
+            parts.append((T[bank][:, CH * c:CH * c + CH], T.IDB[:], T[G][:, 1024 * c + m:1024 * c + 1024:16], whole and m == 0, whole and m == 15))
+        mms(bank, parts, ["%s.%d" % (G, c), "IDB"])
+
+    def kin_gather(out, lst):
+        op("v", ["K", lst], [out], lambda: V.tensor_copy(T[out][:], T.K[:, 0:W].indirect(ap(lst))))
+
+    def scatter_R():
+        op("v", ["NVR", "SL"], ["R"], lambda: V.tensor_copy(T.R[:].indirect(T.SL[:]), T.NVR[:]))
+
+    def update_S(t):
+        mk = "MK%d" % (t % 2)
+        op("v", ["DL", "EXP", mk], ["XS"], lambda: V.tensor_tensor(T.XS[:], T.DL[:].indirect(T.EXP[:]), T[mk][:], Op.mult))
+        tt(S, S, b("XS"), Op.add)
+
+    for t in range(RO):
+        last = t == RO - 1
+        cl = "CL%d" % t
+        kin_gather("KL", cl)
+        act(b("CWF"), ("pM", T.pM[:, 16:32]))
+        op("a", ["X", cl], ["XR"], lambda: A.activation(T.XR[:, 0::16], T.X[:].indirect(ap(cl)), Fn.Copy))
+        op("a", ["IDX", cl], ["CREP"], lambda: A.activation(T.CREP[:], T.IDX[:].indirect(ap(cl)), Fn.Copy))
+        op("a", ["E", cl], ["RCE"], lambda: A.activation(T.RCE[:], T.E[:, 0:W].indirect(ap(cl)), Fn.Copy))
+        for c in range(NCH):
+            if c not in OWN_LAST:
+                rec_piece("a", "GO", "KL", c)
+        mms("pM", [(T.pM[:, 64:80], T.SH[:], T.CC[:], True, False), (T.pM[:, 72:80], T.SHW[:], T.CC[:, 0:8], False, True)], ["SH", "SHW", "CC"])
+        if not last:
+            mms("pM", [(T.pM[:, 32:48], T.PSW[:], T.CWF[:], True, True)], ["PSW", "CWF"])
+        mms("pZ", [(T.pZ[:, 0:L], T.IDB[:], T.RCE[:], True, False)], ["IDB", "RCE"])
+        for c in range(NCH):
+            if c not in OWN_LAST:
+                rec_sum("pZ", "GO", c, False)
+        for st in (8, 4, 2, 1):
+            cp(("XR", T.XR[:, st::2 * st]), ("XR", T.XR[:, 0::2 * st]))
+        if t:
+            update_S(t - 1)
+            scatter_R()
+        cp(b("KCF"), b("KL"))
+        tt(b("DD"), b("CC"), b("LIX"), Op.subtract)
+        for k in range(2):
+            kin_gather("AK%d" % k, "RQ%d%d" % (t, k))
+        mms("pS", [(T.pS[:, 128 * h:128 * h + 128], T.KCF[:, 128 * h:128 * h + 128], T.IDS[:], True, True) for h in range(2)], ["KCF", "IDS"])
+        for c in V_ASK:
+            rec_piece("v", "GA1", "AK1", c)
+        for c in range(NCH):
+            rec_piece("a", "GA0", "AK0", c)
+        for c in V_ASK:
+            rec_sum("pA1", "GA1", c, True)
+        for c in range(NCH):
+            rec_sum("pA0", "GA0", c, True)
+        rest = [c for c in range(NCH) if c not in V_ASK]
+        for n, c in enumerate(rest):
+            rec_piece("a", "GA1", "AK1", c)
+            if n == 0:
+                act(b("AS%d0" % t), ("pA0", T.pA0[:, 0:L]))
+                send_sums(t, 0)
+            rec_sum("pA1", "GA1", c, True)
+        mms("pD", [(T.pD[:, 0:L], T.IDB[:], T.NTH[:], True, False)], ["IDB", "NTH"])
+        o = 0
+        for bb in range(16):
+            n = L - 16 * bb
+            ts(("EQ.%d" % bb, T.EQ[:, o:o + n]), ("CREP", T.CREP[:, 16 * bb:L]), T.CWF[:, bb:bb + 1], None, Op.is_equal, rd=["CWF"])
+            parts = [(T.pD[:, 16 * bb:16 * bb + 16], T.W2[:], T.EQ[:, o:o + 16], False, bb == 15)]
+            if bb < 15:
+                parts.append((T.pD[:, 16 * bb + 16:L], T.W1[:], T.EQ[:, o + 16:o + n], False, False))
+            mms("pD", parts, ["EQ.%d" % bb, "W1", "W2"])
+            o += n
+        if not last:
+            cp(b("SW"), ("pM", T.pM[:, 32:48]))
+            op("a", ["IDX", "SW", "IST%d" % t], ["CSW"], lambda: A.activation(T.CSW[:], T.IDX[:].indirect(T.SW[:]), Fn.Identity, scale=ap("IST%d" % t)))
+            op("a", ["KCF", "NOT%d" % t], ["KVA"], lambda: A.activation(T.KVA[:], T.KCF[:], Fn.Identity, scale=ap("NOT%d" % t)))
+        act(b("AS%d1" % t), ("pA1", T.pA1[:, 0:L]))
+        send_sums(t, 1)
+        for c in OWN_LAST:
+            rec_piece("a", "GO", "KL", c)
+        mms("pK", [(T.pK[:, 0:L], T.O128[:], T.CK[:], True, False)], ["O128", "CK"])
+        for h in range(2):
+            sl = slice(2048 * h, 2048 * h + 2048)
+            op("v", ["X", "KL", "XR"], ["Y.%d" % h], lambda: V.tensor_tensor(T.Y[:, sl], T.X[:].indirect(T.KL[:, 128 * h:128 * h + 128]), T.XR[:, sl], Op.max))
+            parts = []
+            for m in range(16):
+                parts.append((T.pK[:, 128 * h + m:128 * h + 128:16], T.Y[:, 2048 * h + m:2048 * h + 2048:16], T.GB16[:], False, h == 1 and m == 15))
+            mms("pK", parts, ["Y.%d" % h, "GB16"])
+        for c in OWN_LAST:
+            rec_sum("pZ", "GO", c, False)
+        ts(("NT", T.NT[:, 16:16 + L]), ("pD", T.pD[:, 0:L]), 0.0, None, Op.is_ge)
+        op("v", ["R", cl, "TB%d" % t], ["NVR"], lambda: V.tensor_tensor(T.NVR[:], T.R[:, 0:W].indirect(ap(cl)), ap("TB%d" % t), Op.max))
+        if not last:
+            tt(b("KV"), b("KVA"), b("CSW"), Op.add)
+        def fparts(tile, w, fin):
+            return [(T.pF[:, 16 * (s + 1) + 8 * h:16 * (s + 1) + 8 * h + 8], T[tile][:, 16 + 128 * h + 16 * s:144 + 128 * h + 16 * s], T[w][:], False, fin and s == 1 and h == 1)
+                    for s in (-1, 0, 1) for h in range(2)]
+        mms("pF", [(T.pF[:, 0:48], T.IDB[:], T.C48[:], True, False)] + fparts("NT", "GB4", False), ["IDB", "C48", "NT", "GB4"])
+        op("v", ["RST", "pK"], ["RM"], lambda: V.tensor_tensor_scan(T.RM[:], T.RST[:], T.pK[:, 0:L], 0.0, Op.mult, Op.max))
+        tt(b("NI"), ("pK", T.pK[:, 0:L]), b("RM"), Op.not_equal)
+        tt(b("DK"), ("pS", T.pS[:, 0:L]), b("NI"), Op.subtract)
+        op("v", ["NI", "DK"], ["BK"], lambda: V.tensor_tensor_scan(T.BK[:], T.NI[:], T.DK[:], 0.0, Op.mult, Op.max))
+        ts(b("BKF"), ("BK", T.BK[:, 15::16]), 4096.0, None, Op.mult)
+        tt(("D12", T.D12[:, 0:16]), ("pM", T.pM[:, 64:80]), b("BKF"), Op.subtract)
+        tt(("D12", T.D12[:, 16:32]), b("BKF"), b("CC"), Op.subtract)
+        mms("pZ", [(T.pZ[:, 0:L], T.IDB[:], ap("RS%d0" % t), False, False)], ["IDB", "RS%d0" % t])
+        mms("pZ", [(T.pZ[:, 0:L], T.IDB[:], ap("RS%d1" % t), False, True)], ["IDB", "RS%d1" % t])
+        tt(("VT", T.VT[:, 16:16 + L]), ("pZ", T.pZ[:, 0:L]), b("BM%d" % t), Op.is_ge)
+        ts(("UT", T.UT[:, 16:16 + L]), ("pZ", T.pZ[:, 0:L]), 64.0 ** (6 + t), None, Op.is_ge)
+        mms("pF", fparts("VT", "GB32", False), ["VT", "GB32"])
+        mms("pF", fparts("UT", "GB", True), ["UT", "GB"])
+        F = ("pF", T.pF[:, 0:48])
+        ts(b("I48"), F, 12.0, None, Op.is_lt)
+        cp(b("FI"), F)
+        if not last:
+            nt = "CST%d" % (t + 1)
+            mms("pF", [(T.pF[:, 64:66], T.IDB[:], ap(nt), True, False)] +
+                [(T.pF[:, 64:66], T.BD[:], T.I48[:, 16 + q:32:8], False, q == 7) for q in range(8)], ["IDB", nt, "BD", "I48"])
+        tt(b("SLM"), ("I48", T.I48[:, 16:32]), b("DD"), Op.mult)
+        ts(b("Q1"), b("FI"), 80, None, Op.bitwise_and)
+        ts(b("Q2"), b("FI"), 81, None, Op.bitwise_and)
+        expand("LH2", "SLM")
+        mms("pM", [(T.pM[:, 48:64], T.IDF[:], T.LW[:], True, False)] +
+            [(T.pM[:, 48 + 8 * h:56 + 8 * h], T.LH2[:, 128 * h:128 * h + 128], T.GF[:], False, h == 1) for h in range(2)], ["IDF", "LW", "LH2", "GF"])
+        ts(b("TBB"), b("Q1"), 16.0, None, Op.is_equal)
+        ts(b("OBB"), b("Q2"), 1.0, None, Op.is_equal)
+        if not last:
+            place(t + 1)
+        tt(b("TORN"), b("TBB"), b("I48"), Op.max)
+        tt(b("BO"), b("OBB"), b("I48"), Op.is_gt)
+        if not last:
+            sel1(t + 1)
+        tt(b("RMV"), ("BO", T.BO[:, 0:32]), ("TORN", T.TORN[:, 16:48]), Op.mult)
+        tt(b("P2"), ("TORN", T.TORN[:, 16:32]), ("D12", T.D12[:, 16:32]), Op.mult)
+        tt(b("P1"), b("RMV"), b("D12"), Op.mult)
+        if not last:
+            sel2(t + 1)
+        tt(b("DL1"), ("P1", T.P1[:, 0:16]), ("P1", T.P1[:, 16:32]), Op.add)
+        if not last:
+            tt(b("EQP"), b("PL%d" % (t + 1)), b("PL%d" % t), Op.is_equal)
+        tt(b("DL"), b("DL1"), b("P2"), Op.add)
+        cp(b("SL"), ("pM", T.pM[:, 48:64]))
+        if last:
+            scatter_R()
+            deps("a", ["R"], [])
+            A.dma_start(T.yr[:], T.R[:, 0:W]).then_inc(T.sem.stR, 16)
+            update_S(t)
+            cp(b("SF"), S)
+            mms("pK", [(T.pK[:, 128 * h:128 * h + 128], T.SF[:, 128 * h:128 * h + 128], T.IDF[:], True, True) for h in range(2)], ["SF", "IDF"])
+            cp(b("XS"), ("pK", T.pK[:, 0:L]))
+            deps("s", ["XS"], [])
+            g.sync.dma_start(T.ys[:], T.XS[:]).then_inc(T.sem.stS, 16)
+            break
+        for h in range(2):
+            ts(("ED.%d" % h, T.ED[:, 8 * h:8 * h + 8]), ("DL", T.DL[:, 8 * h:8 * h + 8]), T.EQP[:, h:h + 1], None, Op.mult, rd=["EQP"])
+        tt(b("CC"), ("CS", T.CS[:, 15::16]), b("ED"), Op.add, rd=["ED.0", "ED.1"])
+        expand("LH", "CC")
+        wrap(t + 1)
+        op("v", ["RCE", "BT%d" % t, "SL"], ["E"], lambda: V.tensor_tensor(T.E[:].indirect(T.SL[:]), T.RCE[:], ap("BT%d" % t), Op.add))
+        cp(b("CL%d" % (t + 1)), ("pM", T.pM[:, 16:32]))
+        send_list(t + 1)
+        op("v", ["KV", "SL"], ["K"], lambda: V.tensor_copy(T.K[:].indirect(T.SL[:]), T.KV[:]))
+
+    g.wait_ge(T.sem.loc, SWZ["loc"])
+    A.wait_ge(T.sem.stR, 16)
+    g.sync.wait_ge(T.sem.stS, 16)
+    for q in ("v", "a", "p", "q"):
+        g.wait_ge(T.sem[own[q]], cnt[q])

@@ -20,7 +20,6 @@ for _n in ("E", "R"):
 _s("X", W, "bfloat16")
 _s("K", WX, "int32")
 _s("SN", L, "int32")
-_s("SF", L)
 _s("IDX", W)
 for _n in ("GO", "GA0", "GA1", "Y", "XR"):
     _s(_n, 16 * L, "bfloat16")
@@ -47,9 +46,12 @@ _many("BTB", ["BT%d" % t for t in _TT], L, "bfloat16")
 _many("TBF", ["TB%d" % t for t in _TT], L, "bfloat16")
 _many("ISB", ["IST%d" % t for t in _TT], 1)
 _many("NOB2", ["NOT%d" % t for t in _TT], 1)
+_many("DGB", ["DN%d" % t for t in range(3)] + ["DI%d" % t for t in range(3)], 128, "float16")
 _many("CSB", ["CST%d" % t for t in _TT], 2, "bfloat16")
 _many("PLB", ["PL%d" % t for t in _TT], 2)
-for _n in ("CREP", "KCF", "KVA", "CSW", "KV", "RM", "NI", "DK", "BK", "MS", "CS", "LH", "LH2", "XS", "RST", "JF", "BF", "DG", "NOB", "OB"):
+for _n in ("CREP", "KCF", "CSW", "LH", "SF"):
+    _s(_n, L, "float16")
+for _n in ("KV", "RM", "NI", "DK", "BK", "MS", "CS", "LH2", "XS", "RST", "JF", "BF", "DG", "NOB", "OB"):
     _s(_n, L)
 for _n in ("RCE", "NVR", "MK0", "MK1", "NTH", "CK"):
     _s(_n, L, "bfloat16")
@@ -58,13 +60,16 @@ for _n in ("UT", "VT", "NT"):
 _s("D", L, "int32")
 _s("D15", L, "int32")
 _s("CB", 128, "int32")
-for _n in ("IDF", "IDS", "SH", "SHW", "PSW"):
+for _n in ("IDF", "SH", "SHW", "PSW"):
     _s(_n, 128)
+for _n in ("IDH", "IDS"):
+    _s(_n, 128, "float16")
 for _n in ("IDB", "BD", "W1", "W2", "O128", "IOS"):
     _s(_n, 128, "bfloat16")
 _s("GF", 8)
+_s("GH", 8, "float16")
 _s("G8", 8, "int32")
-for _n in ("GB", "GB4", "GB16", "GB32"):
+for _n in ("GBH", "GB4", "GB16", "GB32"):
     _s(_n, 8, "bfloat16")
 _s("PC", 2, "int32")
 _s("PM", 2, "int32")
@@ -90,7 +95,7 @@ for _n in ("FI", "Q1", "Q2"):
     _s(_n, 48, "int32")
 for _n in ("TBB", "TORN", "OBB", "BO"):
     _s(_n, 48)
-for _n in ("pZ", "pA0", "pA1", "pK", "pS", "pD", "pF", "pM"):
+for _n in ("pZ", "pZ2", "pA", "pK", "pS", "pD", "pF", "pM"):
     _s(_n, 512, "float32", "psum")
 
 SEMAPHORES = ["sv", "sa", "sp", "sq", "loc", "ldS", "ldK", "ldR", "ldX", "stR", "stS"]
@@ -129,9 +134,7 @@ def rank_program(g, core, T, topo):
         for k in reads:
             e = entry(k)
             if k[0] == "p":
-                for q2, tok in e["lw"].items():
-                    if not (q2 == q == "p"):
-                        d.append(tok)
+                d += [tok for q2, tok in e["lw"].items() if not (q2 == q == "p")]
                 d += [tok for q2, tok in e["r"].items() if q2 != q]
             elif e["w"]:
                 d.append(e["w"])
@@ -150,7 +153,13 @@ def rank_program(g, core, T, topo):
         for s in best:
             need(q, (s, best[s]))
 
-    def mark(q, tok, reads, writes):
+    def op(q, reads, writes, fn):
+        deps(q, reads, writes)
+        ins = fn()
+        cnt[q] += 1
+        tok = (own[q], cnt[q])
+        ins.then_inc(T.sem[own[q]], 1)
+        snap[tok] = dict(known[q])
         for k in reads:
             entry(k)["r"][q] = tok
         for k in writes:
@@ -160,21 +169,12 @@ def rank_program(g, core, T, topo):
             else:
                 e["w"] = tok
                 e["r"] = {}
-
-    def op(q, reads, writes, fn):
-        deps(q, reads, writes)
-        ins = fn()
-        cnt[q] += 1
-        tok = (own[q], cnt[q])
-        ins.then_inc(T.sem[own[q]], 1)
-        snap[tok] = dict(known[q])
-        mark(q, tok, reads, writes)
         return tok
 
     def landed(k, sem, n):
         entry(k)["w"] = (sem, n)
 
-    def ts(o, i, s1, s2, op0, op1=None, rd=(), wr=None, q="v"):
+    def ts(o, i, s1, s2, op0, op1=None, rd=()):
         (on, oa), (inn, ia) = o, i
         if op1 is None:
             f = lambda: V.tensor_scalar(oa, ia, s1, None, op0)
@@ -227,26 +227,47 @@ def rank_program(g, core, T, topo):
     iota("JF", [[0, 16], [1, 16]], 0, 0, True)
     iota("EXI", [[1, 16]], 0, 0)
     iota("G8", [[1, 8]], 0, 0)
+    iota("CB", [[1, 8], [0, 16]], 0, 0)
+    iota("BF", [[1, 16], [0, 16]], 0, 0, True)
+    iota("LIX", [[128, 2], [0, 8]], W, 1, True)
+    iota("LWB", [[16, 16]], W, 0, True)
+    iota("IDX", [[1, W]], 0, 0, True)
     ts(b("PM"), b("PC"), 15, None, Op.bitwise_and)
-    cp(b("PMF"), b("PM"))
     ts(b("SMI", 0, 1), b("PC", 0, 1), 4, None, Op.arith_shift_right)
+    cp(b("PMF"), b("PM"))
     cp(b("PGF"), b("SMI", 0, 1))
-    ts(b("IDF"), b("D", 0, 128), 0.0, None, Op.is_equal)
-    ts(b("IDB"), b("D", 0, 128), 0.0, None, Op.is_equal)
+    ln2 = math.log(2.0)
+    act(b("P15"), b("PMF", 0, 1), Fn.Exp, scale=-ln2, bias=15.0 * ln2)
+    act(b("NTH"), b("JF"), Fn.Exp, scale=-ln2, bias=16.0 * ln2)
+    for nm in ("IDF", "IDB", "IDH"):
+        ts(b(nm), b("D", 0, 128), 0.0, None, Op.is_equal)
     for t in range(RO):
         ts(b("CST%d" % t), b("PMF"), 5.0, t - 7.5, Op.mult, Op.add)
     ts(b("IOS"), b("JF", 0, 128), -7.5, None, Op.add)
     cp(b("EXP"), b("EXI"))
     ts(b("D15"), b("D"), 15, None, Op.bitwise_and)
+    ts(b("GF"), b("G8"), T.PGF[:, 0:1], None, Op.is_equal, rd=["PGF"])
     ts(b("DG"), b("D15"), 0.0, None, Op.is_equal)
     ts(b("RST"), b("JF"), 1.0, None, Op.min)
-    ts(b("GF"), b("G8"), T.PGF[:, 0:1], None, Op.is_equal, rd=["PGF"])
+    cp(b("GH"), b("GF"))
+    for t in range(RO - 1):
+        ts(b("IST%d" % t), b("PMF", 0, 1), float(t), None, Op.is_equal)
+        ts(b("NOT%d" % t), b("PMF", 0, 1), float(t), None, Op.not_equal)
+    ts(b("BD"), b("CB"), T.PGF[:, 0:1], None, Op.is_equal, rd=["PGF"])
+    for nm, f in (("GBH", 0.5), ("GB4", 4.0), ("GB16", 16.0), ("GB32", 32.0)):
+        ts(b(nm), b("GF"), f, None, Op.mult)
+    ts(b("IDS"), b("IDF"), 1.0 / 4096.0, None, Op.mult)
+    ts(b("SMI", 1, 2), b("PC", 0, 1), 1, None, Op.bitwise_and)
+    fill("O128", 1.0 / 128.0)
+    ts(b("SG"), b("SMI", 1, 2), -2.0, 1.0, Op.mult, Op.add)
+    fill("C48", 12.0)
+    ts(b("PSW"), b("D", 0, 128), T.SG[:, 0:1], None, Op.is_equal, rd=["SG"])
     cp(b("SF"), b("SN"))
     S = ("pS", T.pS[:, 256:512])
-    mms("pS", [(T.pS[:, 256 + 128 * h:384 + 128 * h], T.SF[:, 128 * h:128 * h + 128], T.IDF[:], True, True) for h in range(2)], ["SF", "IDF"])
+    mms("pS", [(T.pS[:, 256 + 128 * h:384 + 128 * h], T.SF[:, 128 * h:128 * h + 128], T.IDH[:], True, True) for h in range(2)], ["SF", "IDH"])
 
     MAG = 1.5 * 2.0 ** 27
-    SWZ = {}
+    LOC = {"n": 0}
 
     def place(t):
         mk = "MK%d" % (t % 2)
@@ -255,8 +276,7 @@ def rank_program(g, core, T, topo):
             ts((mk, T[mk][:, 128 * h:128 * h + 128]), b("IOS"), T.RR[:, h:h + 1], T.pF[:, 64 + h:65 + h], Op.add, Op.is_equal, rd=["RR", "pF"])
 
     def sel1(t):
-        mk = "MK%d" % (t % 2)
-        tt(b("MS"), S, b(mk), Op.mult)
+        tt(b("MS"), S, b("MK%d" % (t % 2)), Op.mult)
 
     def sel2(t):
         op("v", ["RST", "MS"], ["CS"], lambda: V.tensor_tensor_scan(T.CS[:], T.RST[:], T.MS[:], 0.0, Op.mult, Op.add))
@@ -266,14 +286,12 @@ def rank_program(g, core, T, topo):
         op("v", [src, "EXP", "DG"], [out], lambda: V.tensor_tensor(T[out][:], T[src][:].indirect(T.EXP[:]), T.DG[:], Op.mult))
 
     def wrap(t):
-        mms("pM", [(T.pM[:, 16 + 8 * h:24 + 8 * h], T.LH[:, 128 * h:128 * h + 128], T.GF[:], True, True) for h in range(2)], ["LH", "GF"])
+        mms("pM", [(T.pM[:, 16 + 8 * h:24 + 8 * h], T.LH[:, 128 * h:128 * h + 128], T.GH[:], True, True) for h in range(2)], ["LH", "GH"])
 
     def send_list(t):
         trs = []
-        n = 0
         for k in range(2):
-            q = (rank + 1 + ((2 * t + k) % 7)) % NR
-            dst = T.cores[q]
+            dst = T.cores[(rank + 1 + ((2 * t + k) % 7)) % NR]
             es = topo.engines(core, dst)
             half = len(es) // 2
             m = 0
@@ -284,17 +302,16 @@ def rank_program(g, core, T, topo):
                                          src=ap("CL%d" % t), dst=ap("RQ%d%d" % (t, k))))
             a = T.cores[(rank - 1 - ((2 * t + k) % 7)) % NR]
             landed("RQ%d%d" % (t, k), "rq%d%d" % (t, k), len(topo.engines(a, core)) // 2)
-            n += half
+            LOC["n"] += half
         deps("q", ["CL%d" % t], [])
         g.remote_dma_fused(trs, local_sem=T.sem.loc)
-        SWZ["loc"] = SWZ.get("loc", 0) + n
 
     def send_sums(t, k):
         asker = T.cores[(rank - 1 - ((2 * t + k) % 7)) % NR]
         rid, pid, _x = topo.addr(asker)
         deps("q", ["AS%d%d" % (t, k)], [])
         g.remote_dma(ap("RS%d%d" % (t, k)), ap("AS%d%d" % (t, k)), T.sem["rs%d%d" % (t, k)], T.sem.loc, pid, rid, topo.mask(core, asker))
-        SWZ["loc"] += len(topo.engines(core, asker))
+        LOC["n"] += len(topo.engines(core, asker))
         q = T.cores[(rank + 1 + ((2 * t + k) % 7)) % NR]
         landed("RS%d%d" % (t, k), "rs%d%d" % (t, k), len(topo.engines(q, core)))
 
@@ -308,41 +325,25 @@ def rank_program(g, core, T, topo):
     cp(b("CL0"), ("pM", T.pM[:, 16:32]))
     send_list(0)
 
-    iota("CB", [[1, 8], [0, 16]], 0, 0)
-    iota("BF", [[1, 16], [0, 16]], 0, 0, True)
-    iota("LIX", [[128, 2], [0, 8]], W, 1, True)
-    iota("LWB", [[16, 16]], W, 0, True)
-    iota("IDX", [[1, W]], 0, 0, True)
-    ln2 = math.log(2.0)
-    act(b("P15"), b("PMF", 0, 1), Fn.Exp, scale=-ln2, bias=15.0 * ln2)
-    act(b("NTH"), b("JF"), Fn.Exp, scale=-ln2, bias=16.0 * ln2)
     act(("E", T.E[:, 0:W]), ("R", T.R[:, 0:W]), Fn.Exp, scale=6.0 * ln2)
-    ts(b("NTH"), b("NTH"), -1.0, None, Op.mult)
-    ts(b("BD"), b("CB"), T.PGF[:, 0:1], None, Op.is_equal, rd=["PGF"])
-    ts(b("W2"), b("BD"), T.P15[:, 0:1], None, Op.mult, rd=["P15"])
-    ts(b("W1"), b("BD"), 65536.0, None, Op.mult)
-    for nm, f in (("GB", 1.0), ("GB4", 4.0), ("GB16", 16.0), ("GB32", 32.0)):
-        ts(b(nm), b("GF"), f, None, Op.mult)
-    ts(b("IDS"), b("IDF"), 1.0 / 4096.0, None, Op.mult)
+    for t in range(RO - 1):
+        act(b("DN%d" % t), b("IDF"), Fn.Identity, rd=["NOT%d" % t], scale=ap("NOT%d" % t))
+        act(b("DI%d" % t), b("IDF"), Fn.Identity, rd=["IST%d" % t], scale=ap("IST%d" % t))
     ts(b("SH"), b("D", 0, 128), 16.0, None, Op.is_equal)
     ts(b("SHW"), b("D", 0, 128), -112.0, None, Op.is_equal)
-    ts(b("SMI", 1, 2), b("PC", 0, 1), 1, None, Op.bitwise_and)
-    ts(b("SG"), b("SMI", 1, 2), -2.0, 1.0, Op.mult, Op.add)
-    ts(b("PSW"), b("D", 0, 128), T.SG[:, 0:1], None, Op.is_equal, rd=["SG"])
     ts(b("CK"), b("JF"), -1.0, 15.0, Op.mult, Op.add)
-    fill("O128", 1.0 / 128.0)
-    fill("C48", 4.0)
-    for nm, x in (("UT", 0.0), ("VT", 0.0), ("NT", 1.0)):
+    for nm, x in (("UT", -1.0), ("VT", 0.0), ("NT", 1.0)):
         fill(nm, x)
     ts(b("LW"), b("LWB"), T.PMF[:, 0:1], None, Op.add, rd=["PMF"])
+    ts(b("NTH"), b("NTH"), -1.0, None, Op.mult)
+    ts(b("W2"), b("BD"), T.P15[:, 0:1], None, Op.mult, rd=["P15"])
+    ts(b("W1"), b("BD"), 65536.0, None, Op.mult)
     ts(b("NOB"), b("BF"), T.PMF[:, 0:1], None, Op.not_equal, rd=["PMF"])
     ts(b("OB"), b("BF"), T.PMF[:, 0:1], None, Op.is_equal, rd=["PMF"])
     for t in range(RO):
         ts(b("BM%d" % t), b("NOB"), 1e29, 64.0 ** (5 + t), Op.mult, Op.add)
         if t < RO - 1:
             ts(b("BT%d" % t), b("OB"), 64.0 ** (8 + t), None, Op.mult)
-            ts(b("IST%d" % t), b("PMF", 0, 1), float(t), None, Op.is_equal)
-            ts(b("NOT%d" % t), b("PMF", 0, 1), float(t), None, Op.not_equal)
         ts(b("TB%d" % t), b("OB"), float(8 + t), None, Op.mult)
 
     def rec_piece(q, G, lst, c):
@@ -353,11 +354,18 @@ def rank_program(g, core, T, topo):
         else:
             op("v", ["E", lst], [key], lambda: V.tensor_copy(o, T.E[:, 0:W].indirect(off)))
 
-    def rec_sum(bank, G, c, whole):
+    def rec_sum(bank, col, G, c, whole):
         parts = []
         for m in range(16):
-            parts.append((T[bank][:, CH * c:CH * c + CH], T.IDB[:], T[G][:, 1024 * c + m:1024 * c + 1024:16], whole and m == 0, whole and m == 15))
+            parts.append((T[bank][:, col:col + CH], T.IDB[:], T[G][:, 1024 * c + m:1024 * c + 1024:16], whole and m == 0, whole and m == 15))
         mms(bank, parts, ["%s.%d" % (G, c), "IDB"])
+
+    def own_sum(c):
+        rec_sum("pZ2" if c >= NCH // 2 else "pZ", CH * (c % (NCH // 2)), "GO", c, False)
+
+    def both(src, first, fin):
+        for h, z in ((0, "pZ"), (1, "pZ2")):
+            mms(z, [(T[z][:, 0:128], T.IDB[:], ap(src, 128 * h, 128 * h + 128), first, fin)], ["IDB", src])
 
     def kin_gather(out, lst):
         op("v", ["K", lst], [out], lambda: V.tensor_copy(T[out][:], T.K[:, 0:W].indirect(ap(lst))))
@@ -370,10 +378,44 @@ def rank_program(g, core, T, topo):
         op("v", ["DL", "EXP", mk], ["XS"], lambda: V.tensor_tensor(T.XS[:], T.DL[:].indirect(T.EXP[:]), T[mk][:], Op.mult))
         tt(S, S, b("XS"), Op.add)
 
+    def fparts(tile, w, which, fin=False):
+        return [(T.pF[:, 16 * (s + 1) + 8 * h:16 * (s + 1) + 8 * h + 8], T[tile][:, 16 + 128 * h + 16 * s:144 + 128 * h + 16 * s], T[w][:], False, fin and n == len(which) - 1)
+                for n, (h, s) in enumerate(which)]
+
+    LOW, HIGH, MIXED = [(0, -1), (0, 0)], [(1, 0), (1, 1)], [(0, 1), (1, -1)]
+
+    def compare_lanes():
+        o = 0
+        for bb in range(16):
+            n = L - 16 * bb
+            ts(("EQ.%d" % bb, T.EQ[:, o:o + n]), ("CREP", T.CREP[:, 16 * bb:L]), T.CWF[:, bb:bb + 1], None, Op.is_equal, rd=["CWF"])
+            o += n
+
+    def count_lanes(lo, hi):
+        if lo == 0:
+            mms("pD", [(T.pD[:, 0:L], T.IDB[:], T.NTH[:], True, False)], ["IDB", "NTH"])
+        for bb in range(lo, hi):
+            n = L - 16 * bb
+            o = sum(L - 16 * x for x in range(bb))
+            parts = [(T.pD[:, 16 * bb:16 * bb + 16], T.W2[:], T.EQ[:, o:o + 16], False, bb == 15)]
+            if bb < 15:
+                parts.append((T.pD[:, 16 * bb + 16:L], T.W1[:], T.EQ[:, o + 16:o + n], False, False))
+            mms("pD", parts, ["EQ.%d" % bb, "W1", "W2"])
+
+    def best_half(h):
+        sl = slice(2048 * h, 2048 * h + 2048)
+        op("v", ["X", "KL", "XR"], ["Y.%d" % h], lambda: V.tensor_tensor(T.Y[:, sl], T.X[:].indirect(T.KL[:, 128 * h:128 * h + 128]), T.XR[:, sl], Op.max))
+
+    def best_sum(h):
+        parts = []
+        for m in range(16):
+            parts.append((T.pK[:, 128 * h + m:128 * h + 128:16], T.Y[:, 2048 * h + m:2048 * h + 2048:16], T.GB16[:], False, h == 1 and m == 15))
+        mms("pK", parts, ["Y.%d" % h, "GB16"])
+
+    kin_gather("KL", "CL0")
     for t in range(RO):
         last = t == RO - 1
         cl = "CL%d" % t
-        kin_gather("KL", cl)
         act(b("CWF"), ("pM", T.pM[:, 16:32]))
         op("a", ["X", cl], ["XR"], lambda: A.activation(T.XR[:, 0::16], T.X[:].indirect(ap(cl)), Fn.Copy))
         op("a", ["IDX", cl], ["CREP"], lambda: A.activation(T.CREP[:], T.IDX[:].indirect(ap(cl)), Fn.Copy))
@@ -384,71 +426,61 @@ def rank_program(g, core, T, topo):
         mms("pM", [(T.pM[:, 64:80], T.SH[:], T.CC[:], True, False), (T.pM[:, 72:80], T.SHW[:], T.CC[:, 0:8], False, True)], ["SH", "SHW", "CC"])
         if not last:
             mms("pM", [(T.pM[:, 32:48], T.PSW[:], T.CWF[:], True, True)], ["PSW", "CWF"])
-        mms("pZ", [(T.pZ[:, 0:L], T.IDB[:], T.RCE[:], True, False)], ["IDB", "RCE"])
+        both("RCE", True, False)
         for c in range(NCH):
             if c not in OWN_LAST:
-                rec_sum("pZ", "GO", c, False)
+                own_sum(c)
         for st in (8, 4, 2, 1):
             cp(("XR", T.XR[:, st::2 * st]), ("XR", T.XR[:, 0::2 * st]))
-        if t:
-            update_S(t - 1)
-            scatter_R()
         cp(b("KCF"), b("KL"))
         tt(b("DD"), b("CC"), b("LIX"), Op.subtract)
         for k in range(2):
             kin_gather("AK%d" % k, "RQ%d%d" % (t, k))
+        if t:
+            scatter_R()
+            update_S(t - 1)
         mms("pS", [(T.pS[:, 128 * h:128 * h + 128], T.KCF[:, 128 * h:128 * h + 128], T.IDS[:], True, True) for h in range(2)], ["KCF", "IDS"])
         for c in V_ASK:
             rec_piece("v", "GA1", "AK1", c)
         for c in range(NCH):
             rec_piece("a", "GA0", "AK0", c)
         for c in V_ASK:
-            rec_sum("pA1", "GA1", c, True)
-        for c in range(NCH):
-            rec_sum("pA0", "GA0", c, True)
+            rec_sum("pA", L + CH * c, "GA1", c, True)
+        compare_lanes()
+        if not last:
+            cp(b("SW"), ("pM", T.pM[:, 32:48]))
+        best_half(0)
+        for c in range(NCH - 1):
+            rec_sum("pA", CH * c, "GA0", c, True)
+        count_lanes(0, 8)
+        rec_sum("pA", CH * (NCH - 1), "GA0", NCH - 1, True)
+        mms("pK", [(T.pK[:, 0:L], T.O128[:], T.CK[:], True, False)], ["O128", "CK"])
         rest = [c for c in range(NCH) if c not in V_ASK]
         for n, c in enumerate(rest):
             rec_piece("a", "GA1", "AK1", c)
             if n == 0:
-                act(b("AS%d0" % t), ("pA0", T.pA0[:, 0:L]))
+                act(b("AS%d0" % t), ("pA", T.pA[:, 0:L]))
                 send_sums(t, 0)
-            rec_sum("pA1", "GA1", c, True)
-        mms("pD", [(T.pD[:, 0:L], T.IDB[:], T.NTH[:], True, False)], ["IDB", "NTH"])
-        o = 0
-        for bb in range(16):
-            n = L - 16 * bb
-            ts(("EQ.%d" % bb, T.EQ[:, o:o + n]), ("CREP", T.CREP[:, 16 * bb:L]), T.CWF[:, bb:bb + 1], None, Op.is_equal, rd=["CWF"])
-            parts = [(T.pD[:, 16 * bb:16 * bb + 16], T.W2[:], T.EQ[:, o:o + 16], False, bb == 15)]
-            if bb < 15:
-                parts.append((T.pD[:, 16 * bb + 16:L], T.W1[:], T.EQ[:, o + 16:o + n], False, False))
-            mms("pD", parts, ["EQ.%d" % bb, "W1", "W2"])
-            o += n
+                count_lanes(8, 16)
+            rec_sum("pA", L + CH * c, "GA1", c, True)
         if not last:
-            cp(b("SW"), ("pM", T.pM[:, 32:48]))
-            op("a", ["IDX", "SW", "IST%d" % t], ["CSW"], lambda: A.activation(T.CSW[:], T.IDX[:].indirect(T.SW[:]), Fn.Identity, scale=ap("IST%d" % t)))
-            op("a", ["KCF", "NOT%d" % t], ["KVA"], lambda: A.activation(T.KVA[:], T.KCF[:], Fn.Identity, scale=ap("NOT%d" % t)))
-        act(b("AS%d1" % t), ("pA1", T.pA1[:, 0:L]))
+            op("a", ["IDX", "SW"], ["CSW"], lambda: A.activation(T.CSW[:], T.IDX[:].indirect(T.SW[:]), Fn.Copy))
+        act(b("AS%d1" % t), ("pA", T.pA[:, L:2 * L]))
         send_sums(t, 1)
         for c in OWN_LAST:
             rec_piece("a", "GO", "KL", c)
-        mms("pK", [(T.pK[:, 0:L], T.O128[:], T.CK[:], True, False)], ["O128", "CK"])
-        for h in range(2):
-            sl = slice(2048 * h, 2048 * h + 2048)
-            op("v", ["X", "KL", "XR"], ["Y.%d" % h], lambda: V.tensor_tensor(T.Y[:, sl], T.X[:].indirect(T.KL[:, 128 * h:128 * h + 128]), T.XR[:, sl], Op.max))
-            parts = []
-            for m in range(16):
-                parts.append((T.pK[:, 128 * h + m:128 * h + 128:16], T.Y[:, 2048 * h + m:2048 * h + 2048:16], T.GB16[:], False, h == 1 and m == 15))
-            mms("pK", parts, ["Y.%d" % h, "GB16"])
-        for c in OWN_LAST:
-            rec_sum("pZ", "GO", c, False)
+        best_half(1)
+        best_sum(0)
+        best_sum(1)
         ts(("NT", T.NT[:, 16:16 + L]), ("pD", T.pD[:, 0:L]), 0.0, None, Op.is_ge)
-        op("v", ["R", cl, "TB%d" % t], ["NVR"], lambda: V.tensor_tensor(T.NVR[:], T.R[:, 0:W].indirect(ap(cl)), ap("TB%d" % t), Op.max))
         if not last:
-            tt(b("KV"), b("KVA"), b("CSW"), Op.add)
-        def fparts(tile, w, fin):
-            return [(T.pF[:, 16 * (s + 1) + 8 * h:16 * (s + 1) + 8 * h + 8], T[tile][:, 16 + 128 * h + 16 * s:144 + 128 * h + 16 * s], T[w][:], False, fin and s == 1 and h == 1)
-                    for s in (-1, 0, 1) for h in range(2)]
-        mms("pF", [(T.pF[:, 0:48], T.IDB[:], T.C48[:], True, False)] + fparts("NT", "GB4", False), ["IDB", "C48", "NT", "GB4"])
+            mms("pM", [(T.pM[:, 128:128 + L], ap("DN%d" % t), T.KCF[:], True, False), (T.pM[:, 128:128 + L], ap("DI%d" % t), T.CSW[:], False, True)],
+                ["DN%d" % t, "DI%d" % t, "KCF", "CSW"])
+            act(b("KV"), ("pM", T.pM[:, 128:128 + L]))
+        for c in OWN_LAST:
+            own_sum(c)
+        op("v", ["R", cl, "TB%d" % t], ["NVR"], lambda: V.tensor_tensor(T.NVR[:], T.R[:, 0:W].indirect(ap(cl)), ap("TB%d" % t), Op.max))
+        mms("pF", [(T.pF[:, 0:48], T.IDB[:], T.C48[:], True, False)] + fparts("NT", "GB4", LOW + HIGH + MIXED), ["IDB", "C48", "NT", "GB4"])
         op("v", ["RST", "pK"], ["RM"], lambda: V.tensor_tensor_scan(T.RM[:], T.RST[:], T.pK[:, 0:L], 0.0, Op.mult, Op.max))
         tt(b("NI"), ("pK", T.pK[:, 0:L]), b("RM"), Op.not_equal)
         tt(b("DK"), ("pS", T.pS[:, 0:L]), b("NI"), Op.subtract)
@@ -456,12 +488,16 @@ def rank_program(g, core, T, topo):
         ts(b("BKF"), ("BK", T.BK[:, 15::16]), 4096.0, None, Op.mult)
         tt(("D12", T.D12[:, 0:16]), ("pM", T.pM[:, 64:80]), b("BKF"), Op.subtract)
         tt(("D12", T.D12[:, 16:32]), b("BKF"), b("CC"), Op.subtract)
-        mms("pZ", [(T.pZ[:, 0:L], T.IDB[:], ap("RS%d0" % t), False, False)], ["IDB", "RS%d0" % t])
-        mms("pZ", [(T.pZ[:, 0:L], T.IDB[:], ap("RS%d1" % t), False, True)], ["IDB", "RS%d1" % t])
-        tt(("VT", T.VT[:, 16:16 + L]), ("pZ", T.pZ[:, 0:L]), b("BM%d" % t), Op.is_ge)
-        ts(("UT", T.UT[:, 16:16 + L]), ("pZ", T.pZ[:, 0:L]), 64.0 ** (6 + t), None, Op.is_ge)
-        mms("pF", fparts("VT", "GB32", False), ["VT", "GB32"])
-        mms("pF", fparts("UT", "GB", True), ["UT", "GB"])
+        both("RS%d0" % t, False, False)
+        both("RS%d1" % t, False, True)
+        for h, z in ((0, "pZ"), (1, "pZ2")):
+            z2, h2 = ("pZ2", 1) if h == 0 else ("pZ", 0)
+            tt(("VT.%d" % h, T.VT[:, 16 + 128 * h:144 + 128 * h]), (z, T[z][:, 0:128]), b("BM%d" % t, 128 * h, 128 * h + 128), Op.is_ge, rd=["VT"])
+            act(("UT.%d" % h2, T.UT[:, 16 + 128 * h2:144 + 128 * h2]), (z2, T[z2][:, 0:128]), Fn.Sign, rd=["UT"], bias=-0.9 * 64.0 ** (6 + t))
+        mms("pF", fparts("VT", "GB32", LOW), ["VT", "VT.0", "GB32"])
+        mms("pF", fparts("UT", "GBH", HIGH), ["UT", "UT.1", "GBH"])
+        mms("pF", fparts("VT", "GB32", HIGH + MIXED), ["VT", "VT.0", "VT.1", "GB32"])
+        mms("pF", fparts("UT", "GBH", LOW + MIXED, True), ["UT", "UT.0", "UT.1", "GBH"])
         F = ("pF", T.pF[:, 0:48])
         ts(b("I48"), F, 12.0, None, Op.is_lt)
         cp(b("FI"), F)
@@ -499,7 +535,7 @@ def rank_program(g, core, T, topo):
             A.dma_start(T.yr[:], T.R[:, 0:W]).then_inc(T.sem.stR, 16)
             update_S(t)
             cp(b("SF"), S)
-            mms("pK", [(T.pK[:, 128 * h:128 * h + 128], T.SF[:, 128 * h:128 * h + 128], T.IDF[:], True, True) for h in range(2)], ["SF", "IDF"])
+            mms("pK", [(T.pK[:, 128 * h:128 * h + 128], T.SF[:, 128 * h:128 * h + 128], T.IDH[:], True, True) for h in range(2)], ["SF", "IDH"])
             cp(b("XS"), ("pK", T.pK[:, 0:L]))
             deps("s", ["XS"], [])
             g.sync.dma_start(T.ys[:], T.XS[:]).then_inc(T.sem.stS, 16)
@@ -513,8 +549,9 @@ def rank_program(g, core, T, topo):
         cp(b("CL%d" % (t + 1)), ("pM", T.pM[:, 16:32]))
         send_list(t + 1)
         op("v", ["KV", "SL"], ["K"], lambda: V.tensor_copy(T.K[:].indirect(T.SL[:]), T.KV[:]))
+        kin_gather("KL", "CL%d" % (t + 1))
 
-    g.wait_ge(T.sem.loc, SWZ["loc"])
+    g.wait_ge(T.sem.loc, LOC["n"])
     A.wait_ge(T.sem.stR, 16)
     g.sync.wait_ge(T.sem.stS, 16)
     for q in ("v", "a", "p", "q"):

import math
from concourse.bass import DstId, RemoteDMATransfer
from concourse.mybir import dt, AluOpType as Op, ActivationFunctionType as Fn

NR, RO, W, L = 8, 4, 2048, 256
WX = W + L
NCH, CH = 4, 64
V_ASK = (0, 1)
OWN_LAST = (3,)

SCRATCH = {}


def _s(name, cols, dtype="float32", where="sbuf"):
    SCRATCH[name] = (where, [128, cols], dtype)


for _n in ("E", "R"):
    _s(_n, WX, "bfloat16")
_s("X", W, "bfloat16")
_s("K", WX, "int32")
_s("SN", L, "int32")
_s("IDX", W)
for _n in ("GO", "GA0", "GA1", "Y", "XR"):
    _s(_n, 16 * L, "bfloat16")
for _n in ("KL", "AK0", "AK1"):
    _s(_n, L, "uint16")
_s("EQ", 2176, "bfloat16")
LOG = {}


def _many(base, names, cols, dtype="float32"):
    _s(base, cols * len(names), dtype)
    for i, n in enumerate(names):
        LOG[n] = (base, cols * i, cols)


_TT = range(RO)
_TK = [(t, k) for t in range(RO) for k in range(2)]
_many("CLB", ["CL%d" % t for t in _TT], 16, "uint16")
_many("RQB", ["RQ%d%d" % x for x in _TK], 16, "uint16")
_many("RSB", ["RS%d%d" % x for x in _TK], L, "bfloat16")
_many("ASB", ["AS%d%d" % x for x in _TK], L, "bfloat16")
_many("BMB", ["BM%d" % t for t in _TT], L)
_many("BTB", ["BT%d" % t for t in _TT], L, "bfloat16")
_many("TBF", ["TB%d" % t for t in _TT], L, "bfloat16")
_many("ISB", ["IST%d" % t for t in _TT], 1)
_many("NOB2", ["NOT%d" % t for t in _TT], 1)
_many("DGB", ["DN%d" % t for t in range(3)] + ["DI%d" % t for t in range(3)], 128, "float16")
_many("CSB", ["CST%d" % t for t in _TT], 2, "bfloat16")
_many("PLB", ["PL%d" % t for t in _TT], 2)
for _n in ("CREP", "KCF", "CSW", "LH", "SF"):
    _s(_n, L, "float16")
for _n in ("KV", "RM", "NI", "DK", "BK", "MS", "CS", "LH2", "XS", "RST", "JF", "BF", "DG", "NOB", "OB"):
    _s(_n, L)
for _n in ("RCE", "NVR", "MK0", "MK1", "NTH", "CK"):
    _s(_n, L, "bfloat16")
for _n in ("UT", "VT", "NT"):
    _s(_n, L + 32, "bfloat16")
_s("D", L, "int32")
_s("D15", L, "int32")
_s("CB", 128, "int32")
for _n in ("IDF", "SH", "SHW", "PSW"):
    _s(_n, 128)
for _n in ("IDH", "IDS"):
    _s(_n, 128, "float16")
for _n in ("IDB", "BD", "W1", "W2", "O128", "IOS"):
    _s(_n, 128, "bfloat16")
_s("GF", 8)
_s("GH", 8, "float16")
_s("G8", 8, "int32")
for _n in ("GBH", "GB4", "GB16", "GB32"):
    _s(_n, 8, "bfloat16")
_s("PC", 2, "int32")
_s("PM", 2, "int32")
_s("SMI", 8, "int32")
_s("PMF", 2)
_s("PGF", 1)
_s("SG", 1)
_s("P15", 1, "bfloat16")
_s("EXI", 16, "int32")
_s("EXP", 16, "uint16")
_s("SW", 16, "uint16")
_s("SL", 16, "uint16")
for _n in ("LIX", "LWB", "LW", "CWF", "CC", "DD", "SLM", "BKF", "DL", "DL1", "P2", "ED"):
    _s(_n, 16)
_s("D12", 32)
_s("RMV", 32)
_s("P1", 32)
_s("RR", 2)
_s("EQP", 2)
_s("C48", 48, "bfloat16")
_s("I48", 48, "bfloat16")
for _n in ("FI", "Q1", "Q2"):
    _s(_n, 48, "int32")
for _n in ("TBB", "TORN", "OBB", "BO"):
    _s(_n, 48)
for _n in ("pZ", "pZ2", "pA", "pK", "pS", "pD", "pF", "pM"):
    _s(_n, 512, "float32", "psum")

SEMAPHORES = ["sv", "sa", "sp", "sq", "loc", "ldS", "ldK", "ldR", "ldX", "stR", "stS"]
SEMAPHORES += ["rq%d%d" % (t, k) for t in range(RO) for k in range(2)] + ["rs%d%d" % (t, k) for t in range(RO) for k in range(2)]


def rank_program(g, core, T, topo):
    rank = T.rank_of(core)
    if rank is None:
        return
    V, A, PE = g.vector, g.scalar, g.tensor
    eng = {"v": V, "a": A, "p": PE, "q": g, "s": g.sync}
    own = {"v": "sv", "a": "sa", "p": "sp", "q": "sq"}
    cnt = {"v": 0, "a": 0, "p": 0, "q": 0}
    known = {q: {} for q in eng}
    snap = {}
    res = {}

    def need(q, tok):
        s, n = tok
        if known[q].get(s, 0) >= n:
            return
        eng[q].wait_ge(T.sem[s], n)
        known[q][s] = n
        for s2, n2 in snap.get(tok, {}).items():
            if known[q].get(s2, 0) < n2:
                known[q][s2] = n2

    def entry(k):
        if k not in res:
            res[k] = {"w": None, "r": {}, "lw": {}}
        return res[k]

    def deps(q, reads, writes):
        d = []
        for k in reads:
            e = entry(k)
            if k[0] == "p":
                d += [tok for q2, tok in e["lw"].items() if not (q2 == q == "p")]
                d += [tok for q2, tok in e["r"].items() if q2 != q]
            elif e["w"]:
                d.append(e["w"])
        for k in writes:
            e = entry(k)
            if k[0] == "p":
                for m in ("lw", "r"):
                    d += [tok for q2, tok in e[m].items() if not (q2 == q == "p")]
            else:
                if e["w"]:
                    d.append(e["w"])
                d += list(e["r"].values())
        best = {}
        for s, n in d:
            best[s] = max(best.get(s, 0), n)
        for s in best:
            need(q, (s, best[s]))

    def op(q, reads, writes, fn):
        deps(q, reads, writes)
        ins = fn()
        cnt[q] += 1
        tok = (own[q], cnt[q])
        ins.then_inc(T.sem[own[q]], 1)
        snap[tok] = dict(known[q])
        for k in reads:
            entry(k)["r"][q] = tok
        for k in writes:
            e = entry(k)
            if k[0] == "p":
                e["lw"][q] = tok
            else:
                e["w"] = tok
                e["r"] = {}
        return tok

    def landed(k, sem, n):
        entry(k)["w"] = (sem, n)

    def ts(o, i, s1, s2, op0, op1=None, rd=()):
        (on, oa), (inn, ia) = o, i
        if op1 is None:
            f = lambda: V.tensor_scalar(oa, ia, s1, None, op0)
        else:
            f = lambda: V.tensor_scalar(oa, ia, s1, s2, op0, op1)
        return op("v", [inn] + list(rd), [on], f)

    def tt(o, i0, i1, o0, rd=()):
        return op("v", [i0[0], i1[0]] + list(rd), [o[0]], lambda: V.tensor_tensor(o[1], i0[1], i1[1], o0))

    def cp(o, i, rd=()):
        return op("v", [i[0]] + list(rd), [o[0]], lambda: V.tensor_copy(o[1], i[1]))

    def act(o, i, fn=Fn.Copy, rd=(), **kw):
        return op("a", [i[0]] + list(rd), [o[0]], lambda: A.activation(o[1], i[1], fn, **kw))

    def mms(bank, parts, rd):
        def f():
            last = None
            for (oa, l, r, st, sp) in parts:
                last = PE.matmul(oa, l, r, st, sp)
            return last
        return op("p", rd, [bank], f)

    def ap(name, lo=0, hi=None):
        base, o, n = LOG.get(name, (name, 0, SCRATCH[name][1][1] if name in SCRATCH else 0))
        return T[base][:, o + lo:o + (n if hi is None else hi)]

    def b(name, lo=0, hi=None):
        return (name, ap(name, lo, hi))

    def iota(name, pattern, base, cm, imp=False):
        kw = {"allow_small_or_imprecise_dtypes": True} if imp else {}
        return op("q", [], [name], lambda: g.iota(T[name][:], pattern, base, cm, **kw))

    def fill(name, val):
        return op("v", [], [name], lambda: V.memset(ap(name), val))

    g.sync.dma_start(T.SN[:], T.slips[:]).then_inc(T.sem.ldS, 16)
    A.dma_start(T.R[:, 0:W], T.rec[:]).then_inc(T.sem.ldR, 16)
    g.sync.dma_start(T.K[:, 0:W], T.kin[:]).then_inc(T.sem.ldK, 16)
    A.dma_start(T.X[:], T.wealth[:]).then_inc(T.sem.ldX, 16)
    landed("SN", "ldS", 16)
    landed("R", "ldR", 16)
    landed("K", "ldK", 16)
    landed("X", "ldX", 16)

    iota("PC", [[0, 2]], 0, 1)
    iota("D", [[1, L]], 0, -1)
    iota("JF", [[0, 16], [1, 16]], 0, 0, True)
    iota("EXI", [[1, 16]], 0, 0)
    iota("G8", [[1, 8]], 0, 0)
    iota("CB", [[1, 8], [0, 16]], 0, 0)
    iota("BF", [[1, 16], [0, 16]], 0, 0, True)
    iota("LIX", [[128, 2], [0, 8]], W, 1, True)
    iota("LWB", [[16, 16]], W, 0, True)
    iota("IDX", [[1, W]], 0, 0, True)
    ts(b("PM"), b("PC"), 15, None, Op.bitwise_and)
    ts(b("SMI", 0, 1), b("PC", 0, 1), 4, None, Op.arith_shift_right)
    cp(b("PMF"), b("PM"))
    cp(b("PGF"), b("SMI", 0, 1))
    ln2 = math.log(2.0)
    act(b("P15"), b("PMF", 0, 1), Fn.Exp, scale=-ln2, bias=15.0 * ln2)
    act(b("NTH"), b("JF"), Fn.Exp, scale=-ln2, bias=16.0 * ln2)
    for nm in ("IDF", "IDB", "IDH"):
        ts(b(nm), b("D", 0, 128), 0.0, None, Op.is_equal)
    for t in range(RO):
        ts(b("CST%d" % t), b("PMF"), 5.0, t - 7.5, Op.mult, Op.add)
    ts(b("IOS"), b("JF", 0, 128), -7.5, None, Op.add)
    cp(b("EXP"), b("EXI"))
    ts(b("D15"), b("D"), 15, None, Op.bitwise_and)
    ts(b("GF"), b("G8"), T.PGF[:, 0:1], None, Op.is_equal, rd=["PGF"])
    ts(b("DG"), b("D15"), 0.0, None, Op.is_equal)
    ts(b("RST"), b("JF"), 1.0, None, Op.min)
    cp(b("GH"), b("GF"))
    for t in range(RO - 1):
        ts(b("IST%d" % t), b("PMF", 0, 1), float(t), None, Op.is_equal)
        ts(b("NOT%d" % t), b("PMF", 0, 1), float(t), None, Op.not_equal)
    ts(b("BD"), b("CB"), T.PGF[:, 0:1], None, Op.is_equal, rd=["PGF"])
    for nm, f in (("GBH", 0.5), ("GB4", 4.0), ("GB16", 16.0), ("GB32", 32.0)):
        ts(b(nm), b("GF"), f, None, Op.mult)
    ts(b("IDS"), b("IDF"), 1.0 / 4096.0, None, Op.mult)
    ts(b("SMI", 1, 2), b("PC", 0, 1), 1, None, Op.bitwise_and)
    fill("O128", 1.0 / 128.0)
    ts(b("SG"), b("SMI", 1, 2), -2.0, 1.0, Op.mult, Op.add)
    fill("C48", 12.0)
    ts(b("PSW"), b("D", 0, 128), T.SG[:, 0:1], None, Op.is_equal, rd=["SG"])
    cp(b("SF"), b("SN"))
    S = ("pS", T.pS[:, 256:512])
    mms("pS", [(T.pS[:, 256 + 128 * h:384 + 128 * h], T.SF[:, 128 * h:128 * h + 128], T.IDH[:], True, True) for h in range(2)], ["SF", "IDH"])

    MAG = 1.5 * 2.0 ** 27
    LOC = {"n": 0}

    def place(t):
        mk = "MK%d" % (t % 2)
        ts(b("RR"), ("pF", T.pF[:, 64:66]), MAG, -MAG, Op.add, Op.add)
        for h in range(2):
            ts((mk, T[mk][:, 128 * h:128 * h + 128]), b("IOS"), T.RR[:, h:h + 1], T.pF[:, 64 + h:65 + h], Op.add, Op.is_equal, rd=["RR", "pF"])

    def sel1(t):
        tt(b("MS"), S, b("MK%d" % (t % 2)), Op.mult)

    def sel2(t):
        op("v", ["RST", "MS"], ["CS"], lambda: V.tensor_tensor_scan(T.CS[:], T.RST[:], T.MS[:], 0.0, Op.mult, Op.add))
        tt(b("PL%d" % t), ("pF", T.pF[:, 64:66]), b("RR"), Op.subtract)

    def expand(out, src):
        op("v", [src, "EXP", "DG"], [out], lambda: V.tensor_tensor(T[out][:], T[src][:].indirect(T.EXP[:]), T.DG[:], Op.mult))

    def wrap(t):
        mms("pM", [(T.pM[:, 16 + 8 * h:24 + 8 * h], T.LH[:, 128 * h:128 * h + 128], T.GH[:], True, True) for h in range(2)], ["LH", "GH"])

    def send_list(t):
        trs = []
        for k in range(2):
            dst = T.cores[(rank + 1 + ((2 * t + k) % 7)) % NR]
            es = topo.engines(core, dst)
            half = len(es) // 2
            m = 0
            for e in es[k * half:(k + 1) * half]:
                m |= 1 << e
            rid, pid, _x = topo.addr(dst)
            trs.append(RemoteDMATransfer(dst_ids=[DstId(rid=rid, pnc=pid)], dma_engine_mask=m, remote_sem=T.sem["rq%d%d" % (t, k)],
                                         src=ap("CL%d" % t), dst=ap("RQ%d%d" % (t, k))))
            a = T.cores[(rank - 1 - ((2 * t + k) % 7)) % NR]
            landed("RQ%d%d" % (t, k), "rq%d%d" % (t, k), len(topo.engines(a, core)) // 2)
            LOC["n"] += half
        deps("q", ["CL%d" % t], [])
        g.remote_dma_fused(trs, local_sem=T.sem.loc)

    def send_sums(t, k):
        asker = T.cores[(rank - 1 - ((2 * t + k) % 7)) % NR]
        rid, pid, _x = topo.addr(asker)
        deps("q", ["AS%d%d" % (t, k)], [])
        g.remote_dma(ap("RS%d%d" % (t, k)), ap("AS%d%d" % (t, k)), T.sem["rs%d%d" % (t, k)], T.sem.loc, pid, rid, topo.mask(core, asker))
        LOC["n"] += len(topo.engines(core, asker))
        q = T.cores[(rank + 1 + ((2 * t + k) % 7)) % NR]
        landed("RS%d%d" % (t, k), "rs%d%d" % (t, k), len(topo.engines(q, core)))

    mms("pF", [(T.pF[:, 64:66], T.IDB[:], ap("CST0"), True, True)], ["IDB", "CST0"])
    place(0)
    sel1(0)
    sel2(0)
    cp(b("CC"), ("CS", T.CS[:, 15::16]))
    expand("LH", "CC")
    wrap(0)
    cp(b("CL0"), ("pM", T.pM[:, 16:32]))
    send_list(0)

    act(("E", T.E[:, 0:W]), ("R", T.R[:, 0:W]), Fn.Exp, scale=6.0 * ln2)
    for t in range(RO - 1):
        act(b("DN%d" % t), b("IDF"), Fn.Identity, rd=["NOT%d" % t], scale=ap("NOT%d" % t))
        act(b("DI%d" % t), b("IDF"), Fn.Identity, rd=["IST%d" % t], scale=ap("IST%d" % t))
    ts(b("SH"), b("D", 0, 128), 16.0, None, Op.is_equal)
    ts(b("SHW"), b("D", 0, 128), -112.0, None, Op.is_equal)
    ts(b("CK"), b("JF"), -1.0, 15.0, Op.mult, Op.add)
    for nm, x in (("UT", -1.0), ("VT", 0.0), ("NT", 1.0)):
        fill(nm, x)
    ts(b("LW"), b("LWB"), T.PMF[:, 0:1], None, Op.add, rd=["PMF"])
    ts(b("NTH"), b("NTH"), -1.0, None, Op.mult)
    ts(b("W2"), b("BD"), T.P15[:, 0:1], None, Op.mult, rd=["P15"])
    ts(b("W1"), b("BD"), 65536.0, None, Op.mult)
    ts(b("NOB"), b("BF"), T.PMF[:, 0:1], None, Op.not_equal, rd=["PMF"])
    ts(b("OB"), b("BF"), T.PMF[:, 0:1], None, Op.is_equal, rd=["PMF"])
    for t in range(RO):
        ts(b("BM%d" % t), b("NOB"), 1e29, 64.0 ** (5 + t), Op.mult, Op.add)
        if t < RO - 1:
            ts(b("BT%d" % t), b("OB"), 64.0 ** (8 + t), None, Op.mult)
        ts(b("TB%d" % t), b("OB"), float(8 + t), None, Op.mult)

    def rec_piece(q, G, lst, c):
        o, off = T[G][:, 1024 * c:1024 * c + 1024], T[lst][:, CH * c:CH * c + CH]
        key = "%s.%d" % (G, c)
        if q == "a":
            op("a", ["E", lst], [key], lambda: A.activation(o, T.E[:, 0:W].indirect(off), Fn.Copy))
        else:
            op("v", ["E", lst], [key], lambda: V.tensor_copy(o, T.E[:, 0:W].indirect(off)))

    def rec_sum(bank, col, G, c, whole):
        parts = []
        for m in range(16):
            parts.append((T[bank][:, col:col + CH], T.IDB[:], T[G][:, 1024 * c + m:1024 * c + 1024:16], whole and m == 0, whole and m == 15))
        mms(bank, parts, ["%s.%d" % (G, c), "IDB"])

    def own_sum(c):
        rec_sum("pZ2" if c >= NCH // 2 else "pZ", CH * (c % (NCH // 2)), "GO", c, False)

    def both(src, first, fin):
        for h, z in ((0, "pZ"), (1, "pZ2")):
            mms(z, [(T[z][:, 0:128], T.IDB[:], ap(src, 128 * h, 128 * h + 128), first, fin)], ["IDB", src])

    def kin_gather(out, lst):
        op("v", ["K", lst], [out], lambda: V.tensor_copy(T[out][:], T.K[:, 0:W].indirect(ap(lst))))

    def scatter_R():
        op("v", ["NVR", "SL"], ["R"], lambda: V.tensor_copy(T.R[:].indirect(T.SL[:]), T.NVR[:]))

    def update_S(t):
        mk = "MK%d" % (t % 2)
        op("v", ["DL", "EXP", mk], ["XS"], lambda: V.tensor_tensor(T.XS[:], T.DL[:].indirect(T.EXP[:]), T[mk][:], Op.mult))
        tt(S, S, b("XS"), Op.add)

    def fparts(tile, w, which, fin=False):
        return [(T.pF[:, 16 * (s + 1) + 8 * h:16 * (s + 1) + 8 * h + 8], T[tile][:, 16 + 128 * h + 16 * s:144 + 128 * h + 16 * s], T[w][:], False, fin and n == len(which) - 1)
                for n, (h, s) in enumerate(which)]

    LOW, HIGH, MIXED = [(0, -1), (0, 0)], [(1, 0), (1, 1)], [(0, 1), (1, -1)]

    def compare_lanes():
        o = 0
        for bb in range(16):
            n = L - 16 * bb
            ts(("EQ.%d" % bb, T.EQ[:, o:o + n]), ("CREP", T.CREP[:, 16 * bb:L]), T.CWF[:, bb:bb + 1], None, Op.is_equal, rd=["CWF"])
            o += n

    def count_lanes(lo, hi):
        if lo == 0:
            mms("pD", [(T.pD[:, 0:L], T.IDB[:], T.NTH[:], True, False)], ["IDB", "NTH"])
        for bb in range(lo, hi):
            n = L - 16 * bb
            o = sum(L - 16 * x for x in range(bb))
            parts = [(T.pD[:, 16 * bb:16 * bb + 16], T.W2[:], T.EQ[:, o:o + 16], False, bb == 15)]
            if bb < 15:
                parts.append((T.pD[:, 16 * bb + 16:L], T.W1[:], T.EQ[:, o + 16:o + n], False, False))
            mms("pD", parts, ["EQ.%d" % bb, "W1", "W2"])

    def best_half(h):
        sl = slice(2048 * h, 2048 * h + 2048)
        op("v", ["X", "KL", "XR"], ["Y.%d" % h], lambda: V.tensor_tensor(T.Y[:, sl], T.X[:].indirect(T.KL[:, 128 * h:128 * h + 128]), T.XR[:, sl], Op.max))

    def best_sum(h):
        parts = []
        for m in range(16):
            parts.append((T.pK[:, 128 * h + m:128 * h + 128:16], T.Y[:, 2048 * h + m:2048 * h + 2048:16], T.GB16[:], False, h == 1 and m == 15))
        mms("pK", parts, ["Y.%d" % h, "GB16"])

    kin_gather("KL", "CL0")
    for t in range(RO):
        last = t == RO - 1
        cl = "CL%d" % t
        act(b("CWF"), ("pM", T.pM[:, 16:32]))
        op("a", ["X", cl], ["XR"], lambda: A.activation(T.XR[:, 0::16], T.X[:].indirect(ap(cl)), Fn.Copy))
        op("a", ["IDX", cl], ["CREP"], lambda: A.activation(T.CREP[:], T.IDX[:].indirect(ap(cl)), Fn.Copy))
        op("a", ["E", cl], ["RCE"], lambda: A.activation(T.RCE[:], T.E[:, 0:W].indirect(ap(cl)), Fn.Copy))
        for c in range(NCH):
            if c not in OWN_LAST:
                rec_piece("a", "GO", "KL", c)
        mms("pM", [(T.pM[:, 64:80], T.SH[:], T.CC[:], True, False), (T.pM[:, 72:80], T.SHW[:], T.CC[:, 0:8], False, True)], ["SH", "SHW", "CC"])
        if not last:
            mms("pM", [(T.pM[:, 32:48], T.PSW[:], T.CWF[:], True, True)], ["PSW", "CWF"])
        both("RCE", True, False)
        for c in range(NCH):
            if c not in OWN_LAST:
                own_sum(c)
        for st in (8, 4, 2, 1):
            cp(("XR", T.XR[:, st::2 * st]), ("XR", T.XR[:, 0::2 * st]))
        cp(b("KCF"), b("KL"))
        tt(b("DD"), b("CC"), b("LIX"), Op.subtract)
        for k in range(2):
            kin_gather("AK%d" % k, "RQ%d%d" % (t, k))
        if t:
            scatter_R()
            update_S(t - 1)
        mms("pS", [(T.pS[:, 128 * h:128 * h + 128], T.KCF[:, 128 * h:128 * h + 128], T.IDS[:], True, True) for h in range(2)], ["KCF", "IDS"])
        for c in V_ASK:
            rec_piece("v", "GA1", "AK1", c)
        for c in range(NCH):
            rec_piece("a", "GA0", "AK0", c)
        for c in V_ASK:
            rec_sum("pA", L + CH * c, "GA1", c, True)
        compare_lanes()
        if not last:
            cp(b("SW"), ("pM", T.pM[:, 32:48]))
        best_half(0)
        for c in range(NCH - 1):
            rec_sum("pA", CH * c, "GA0", c, True)
        count_lanes(0, 8)
        rec_sum("pA", CH * (NCH - 1), "GA0", NCH - 1, True)
        mms("pK", [(T.pK[:, 0:L], T.O128[:], T.CK[:], True, False)], ["O128", "CK"])
        rest = [c for c in range(NCH) if c not in V_ASK]
        for n, c in enumerate(rest):
            rec_piece("a", "GA1", "AK1", c)
            if n == 0:
                act(b("AS%d0" % t), ("pA", T.pA[:, 0:L]))
                send_sums(t, 0)
                count_lanes(8, 16)
            rec_sum("pA", L + CH * c, "GA1", c, True)
        if not last:
            op("a", ["IDX", "SW"], ["CSW"], lambda: A.activation(T.CSW[:], T.IDX[:].indirect(T.SW[:]), Fn.Copy))
        act(b("AS%d1" % t), ("pA", T.pA[:, L:2 * L]))
        send_sums(t, 1)
        for c in OWN_LAST:
            rec_piece("a", "GO", "KL", c)
        best_half(1)
        best_sum(0)
        best_sum(1)
        ts(("NT", T.NT[:, 16:16 + L]), ("pD", T.pD[:, 0:L]), 0.0, None, Op.is_ge)
        if not last:
            mms("pM", [(T.pM[:, 128:128 + L], ap("DN%d" % t), T.KCF[:], True, False), (T.pM[:, 128:128 + L], ap("DI%d" % t), T.CSW[:], False, True)],
                ["DN%d" % t, "DI%d" % t, "KCF", "CSW"])
            act(b("KV"), ("pM", T.pM[:, 128:128 + L]))
        for c in OWN_LAST:
            own_sum(c)
        op("v", ["R", cl, "TB%d" % t], ["NVR"], lambda: V.tensor_tensor(T.NVR[:], T.R[:, 0:W].indirect(ap(cl)), ap("TB%d" % t), Op.max))
        mms("pF", [(T.pF[:, 0:48], T.IDB[:], T.C48[:], True, False)] + fparts("NT", "GB4", LOW + HIGH + MIXED), ["IDB", "C48", "NT", "GB4"])
        op("v", ["RST", "pK"], ["RM"], lambda: V.tensor_tensor_scan(T.RM[:], T.RST[:], T.pK[:, 0:L], 0.0, Op.mult, Op.max))
        tt(b("NI"), ("pK", T.pK[:, 0:L]), b("RM"), Op.not_equal)
        tt(b("DK"), ("pS", T.pS[:, 0:L]), b("NI"), Op.subtract)
        op("v", ["NI", "DK"], ["BK"], lambda: V.tensor_tensor_scan(T.BK[:], T.NI[:], T.DK[:], 0.0, Op.mult, Op.max))
        ts(b("BKF"), ("BK", T.BK[:, 15::16]), 4096.0, None, Op.mult)
        tt(("D12", T.D12[:, 0:16]), ("pM", T.pM[:, 64:80]), b("BKF"), Op.subtract)
        tt(("D12", T.D12[:, 16:32]), b("BKF"), b("CC"), Op.subtract)
        both("RS%d0" % t, False, False)
        both("RS%d1" % t, False, True)
        for h, z in ((0, "pZ"), (1, "pZ2")):
            z2, h2 = ("pZ2", 1) if h == 0 else ("pZ", 0)
            tt(("VT.%d" % h, T.VT[:, 16 + 128 * h:144 + 128 * h]), (z, T[z][:, 0:128]), b("BM%d" % t, 128 * h, 128 * h + 128), Op.is_ge, rd=["VT"])
            act(("UT.%d" % h2, T.UT[:, 16 + 128 * h2:144 + 128 * h2]), (z2, T[z2][:, 0:128]), Fn.Sign, rd=["UT"], bias=-0.9 * 64.0 ** (6 + t))
        mms("pF", fparts("VT", "GB32", LOW), ["VT", "VT.0", "GB32"])
        mms("pF", fparts("UT", "GBH", HIGH), ["UT", "UT.1", "GBH"])
        mms("pF", fparts("VT", "GB32", HIGH + MIXED), ["VT", "VT.0", "VT.1", "GB32"])
        mms("pF", fparts("UT", "GBH", LOW + MIXED, True), ["UT", "UT.0", "UT.1", "GBH"])
        F = ("pF", T.pF[:, 0:48])
        ts(b("I48"), F, 12.0, None, Op.is_lt)
        cp(b("FI"), F)
        if not last:
            nt = "CST%d" % (t + 1)
            mms("pF", [(T.pF[:, 64:66], T.IDB[:], ap(nt), True, False)] +
                [(T.pF[:, 64:66], T.BD[:], T.I48[:, 16 + q:32:8], False, q == 7) for q in range(8)], ["IDB", nt, "BD", "I48"])
        tt(b("SLM"), ("I48", T.I48[:, 16:32]), b("DD"), Op.mult)
        ts(b("Q1"), b("FI"), 80, None, Op.bitwise_and)
        ts(b("Q2"), b("FI"), 81, None, Op.bitwise_and)
        expand("LH2", "SLM")
        mms("pM", [(T.pM[:, 48:64], T.IDF[:], T.LW[:], True, False)] +
            [(T.pM[:, 48 + 8 * h:56 + 8 * h], T.LH2[:, 128 * h:128 * h + 128], T.GF[:], False, h == 1) for h in range(2)], ["IDF", "LW", "LH2", "GF"])
        ts(b("TBB"), b("Q1"), 16.0, None, Op.is_equal)
        ts(b("OBB"), b("Q2"), 1.0, None, Op.is_equal)
        if not last:
            place(t + 1)
        tt(b("TORN"), b("TBB"), b("I48"), Op.max)
        tt(b("BO"), b("OBB"), b("I48"), Op.is_gt)
        if not last:
            sel1(t + 1)
        tt(b("RMV"), ("BO", T.BO[:, 0:32]), ("TORN", T.TORN[:, 16:48]), Op.mult)
        tt(b("P2"), ("TORN", T.TORN[:, 16:32]), ("D12", T.D12[:, 16:32]), Op.mult)
        tt(b("P1"), b("RMV"), b("D12"), Op.mult)
        if not last:
            sel2(t + 1)
        tt(b("DL1"), ("P1", T.P1[:, 0:16]), ("P1", T.P1[:, 16:32]), Op.add)
        if not last:
            tt(b("EQP"), b("PL%d" % (t + 1)), b("PL%d" % t), Op.is_equal)
        tt(b("DL"), b("DL1"), b("P2"), Op.add)
        cp(b("SL"), ("pM", T.pM[:, 48:64]))
        if last:
            scatter_R()
            deps("a", ["R"], [])
            A.dma_start(T.yr[:], T.R[:, 0:W]).then_inc(T.sem.stR, 16)
            update_S(t)
            cp(b("SF"), S)
            mms("pK", [(T.pK[:, 128 * h:128 * h + 128], T.SF[:, 128 * h:128 * h + 128], T.IDH[:], True, True) for h in range(2)], ["SF", "IDH"])
            cp(b("XS"), ("pK", T.pK[:, 0:L]))
            deps("s", ["XS"], [])
            g.sync.dma_start(T.ys[:], T.XS[:]).then_inc(T.sem.stS, 16)
            break
        for h in range(2):
            ts(("ED.%d" % h, T.ED[:, 8 * h:8 * h + 8]), ("DL", T.DL[:, 8 * h:8 * h + 8]), T.EQP[:, h:h + 1], None, Op.mult, rd=["EQP"])
        tt(b("CC"), ("CS", T.CS[:, 15::16]), b("ED"), Op.add, rd=["ED.0", "ED.1"])
        expand("LH", "CC")
        wrap(t + 1)
        op("v", ["RCE", "BT%d" % t, "SL"], ["E"], lambda: V.tensor_tensor(T.E[:].indirect(T.SL[:]), T.RCE[:], ap("BT%d" % t), Op.add))
        cp(b("CL%d" % (t + 1)), ("pM", T.pM[:, 16:32]))
        send_list(t + 1)
        op("v", ["KV", "SL"], ["K"], lambda: V.tensor_copy(T.K[:].indirect(T.SL[:]), T.KV[:]))
        kin_gather("KL", "CL%d" % (t + 1))

    g.wait_ge(T.sem.loc, LOC["n"])
    A.wait_ge(T.sem.stR, 16)
    g.sync.wait_ge(T.sem.stS, 16)
    for q in ("v", "a", "p", "q"):
        g.wait_ge(T.sem[own[q]], cnt[q])
